import numpy as np
import ml_dtypes


def mxq(x, axis, fmt="e4m3"):
    dtype, down = {"e4m3": (ml_dtypes.float8_e4m3fn, 7), "e5m2": (ml_dtypes.float8_e5m2, 14)}[fmt]
    v = np.moveaxis(np.asarray(x, np.float32).astype(ml_dtypes.bfloat16).astype(np.float64), axis, -1)
    blocks = v.reshape(v.shape[:-1] + (-1, 32))
    amax = np.abs(blocks).max(-1, keepdims=True)
    byte = np.maximum(np.where(amax > 0, np.frexp(amax)[1] - 1 + 127, 0) - down, 1)
    scale = np.exp2(byte - 127.0)
    codes = (blocks / scale).astype(np.float32).astype(dtype).astype(np.float64)
    return np.moveaxis((codes * scale).reshape(v.shape), -1, axis)


WIDE = False


def mx_kscale(k):
    if not WIDE:
        return np.ones(k)
    levels = np.array([10, -10, 5, -5, 0])
    if k % 512:
        return np.exp2(np.random.permutation(np.resize(levels, k // 32))).repeat(32)
    a = np.empty((k // 512, 16))
    for p in range(k // 512):
        a[p, :8] = np.random.permutation(np.resize(levels, 8))
        for g in range(8):
            far = levels[np.abs(levels - a[p, g]) >= 10]
            a[p, g + 8] = far[np.random.randint(len(far))]
    return np.exp2(a.ravel()).repeat(32)


BF16 = ml_dtypes.bfloat16


def bf(x):
    return np.asarray(x, np.float32).astype(BF16)


def f64(x):
    return np.asarray(x).astype(np.float64)


E2M1 = np.array([0.0, 0.5, 1.0, 1.5, 2.0, 3.0, 4.0, 6.0, -0.0, -0.5, -1.0, -1.5, -2.0, -3.0, -4.0, -6.0])


def pack_weight(w, fmt):
    k, n = w.shape
    w = f64(bf(w)).reshape(k // 32, 32, n)
    amax = np.abs(w).max(1)
    if fmt == "e4m3":
        byte = np.frexp(amax)[1] - 1 + 127 - 7
    else:
        mant, ex = np.frexp(amax / 6.0)
        byte = np.where(mant > 0.5, ex, ex - 1) + 127
    byte = np.clip(np.where(amax > 0, byte, 1), 1, 254)
    scaled = (w * np.exp2(127.0 - byte)[:, None, :]).reshape(k, n).astype(np.float32)
    by_word = np.ascontiguousarray(scaled.reshape(k // 512, 128, 4, n).transpose(0, 1, 3, 2))
    if fmt == "e4m3":
        words = by_word.astype(ml_dtypes.float8_e4m3fn).view(np.uint8)
    else:
        c = by_word.astype(ml_dtypes.float4_e2m1fn).view(np.uint8) & 0xF
        words = c[..., 0::2] | (c[..., 1::2] << 4)
    return np.ascontiguousarray(words), np.ascontiguousarray(byte.astype(np.uint8).reshape(k // 512, 16, n))


def unpack_weight(words, scales, fmt):
    g, p, n, _ = words.shape
    if fmt == "e4m3":
        vals = np.ascontiguousarray(words).view(ml_dtypes.float8_e4m3fn).astype(np.float64)
    else:
        nib = np.empty((g, p, n, 4), np.uint8)
        nib[..., 0::2] = words & 0xF
        nib[..., 1::2] = words >> 4
        vals = E2M1[nib]
    vals = vals * np.repeat(np.exp2(scales.astype(np.float64) - 127.0), 8, axis=1)[..., None]
    return vals.transpose(0, 1, 3, 2).reshape(g * 512, n)
def pack4(w):
    words, scales = pack_weight(w, "e2m1")
    return words.reshape(words.shape[0], 128, -1), scales


def unpack4(words, scales):
    return unpack_weight(words.reshape(words.shape[0], 128, -1, 2), scales, "e2m1")


def planes(Y):
    n, m = Y.shape
    b = f64(bf(Y)).reshape(n // 32, 32, m)
    amax = np.abs(b).max(1)
    byte = np.clip(np.where(amax > 0, np.frexp(amax)[1] - 1 + 127 - 7, 1), 1, 254)
    codes = (b * np.exp2(127.0 - byte)[:, None, :]).reshape(n, m).astype(np.float32).astype(ml_dtypes.float8_e4m3fn).view(np.uint8)
    words = codes.reshape(n // 512, 128, 4, m).transpose(0, 1, 3, 2)
    return np.ascontiguousarray(words), np.ascontiguousarray(byte.astype(np.uint8).reshape(n // 512, 16, m))


R, G = 1536, 1024
TAU = 0.0125


def setup_inputs():
    s = mx_kscale(R)
    t = mx_kscale(G)
    X = np.random.randn(R, G)
    pos = np.random.rand(R, 2)
    d2 = ((pos[:, None, :] - pos[None, :, :]) ** 2).sum(-1)
    H = np.exp(-d2 / (4 * TAU)) / np.sqrt(2 * np.pi * TAU * R)
    x_words, x_scales = pack_weight(X * s[:, None], "e4m3")
    heat_words, heat_scales = pack4(H / s[:, None])
    infectivity = bf(np.exp(0.3 * np.random.randn(G)) * t)
    contacts = bf(np.exp(0.8 * np.random.randn(G, G)) / np.sqrt(G) / t[:, None])
    imports = bf(0.5 * np.random.randn(G))
    recovery = bf(np.exp(0.8 * np.random.randn(R)))
    return {"x_words": x_words, "x_scales": x_scales,
            "heat_words": heat_words, "heat_scales": heat_scales,
            "infectivity": infectivity, "contacts": contacts,
            "imports": imports, "recovery": recovery}


def reference(x_words, x_scales, heat_words, heat_scales, infectivity, contacts, imports, recovery):
    X = unpack_weight(x_words, x_scales, "e4m3")
    H = unpack4(heat_words, heat_scales)
    D = H.T @ X
    Z = np.tanh(D) * f64(infectivity)[None, :]
    P = mxq(Z, 1, "e4m3") @ mxq(f64(contacts), 0, "e4m3")
    y = (P + f64(imports)[None, :]) * f64(recovery)[:, None]
    Y = y
    words, scales = planes(Y)
    return y, words, scales

@@ -1,0 +1,346 @@
+from contextlib import ExitStack
+
+import concourse.mybir as mybir
+from concourse.masks import make_identity
+
+R, G = 1536, 1024
+FLOPS = 2 * R * R * G + 2 * R * G * G
+
+F32 = mybir.dt.float32
+BF16 = mybir.dt.bfloat16
+I32 = mybir.dt.int32
+U8 = mybir.dt.uint8
+FP8X4 = mybir.dt.float8_e4m3fn_x4
+FP4X4 = mybir.dt.float4_e2m1fn_x4
+ACT = mybir.ActivationFunctionType
+ALU = mybir.AluOpType
+
+P = 128
+PB = 4
+DB = 4
+W = 512
+NR = R // W
+NG = G // W
+
+
+def tile_heat_contact_step_h2_kernel(tc, x_words, x_scales, heat_words, heat_scales,
+                                                infectivity, contacts, imports, recovery,
+                                                out_0, out_1, out_2):
+    nc = tc.nc
+    with ExitStack() as ctx:
+        keep = ctx.enter_context(tc.tile_pool(name="keep", bufs=1))
+        flow = ctx.enter_context(tc.tile_pool(name="flow", bufs=2))
+        psum = ctx.enter_context(tc.psum_pool(name="psum", bufs=4))
+        ctx.enter_context(tc.manual_schedule())
+
+        def kt(name, shape, dt):
+            return keep.tile(shape, dt, name=name, align_bytes=64)
+
+        ident = kt("ident", [P, P], BF16)
+        warm = kt("warm", [P, 16], F32)
+        imp_col = kt("imp_col", [P, 8], BF16)
+        imp_row = kt("imp_row", [P, G], BF16)
+        rec_raw = kt("rec_raw", [P, NR, 16], BF16)
+        rec = kt("rec", [P, NR, 4], F32)
+        inf_raw = kt("inf_raw", [P, 8, 16], BF16)
+        inf = kt("inf", [P, NG, 4, 4], F32)
+        xs_raw = kt("xs_raw", [P, NR, G], U8)
+        xs = [kt("xs%d" % h, [P, NR, W], U8) for h in range(NG)]
+        xw_raw = [kt("xw_raw%d" % h, [P, NR, W], I32) for h in range(NG)]
+        xw = [kt("xw%d" % h, [P, NR, W], I32) for h in range(NG)]
+        hw = [kt("hw%d" % g, [P, NR, 2 * W], U8) for g in range(NR)]
+        hs0 = kt("hs0", [P, NR, W], U8)
+        hs12 = kt("hs12", [P, NR, 2 * W], U8)
+        c_raw = {(h, b): kt("c_raw%d%d" % (h, b), [P, 4, W], BF16) for h in range(NG) for b in range(NG)}
+        cw = {(h, b): kt("cw%d%d" % (h, b), [P, W], I32) for h in range(NG) for b in range(NG)}
+        cs = {(h, b): kt("cs%d%d" % (h, b), [P, W], U8) for h in range(NG) for b in range(NG)}
+        zw = {(g, h): kt("zw%d%d" % (g, h), [P, W], I32) for g in range(NR) for h in range(NG)}
+        zs = {(g, h): kt("zs%d%d" % (g, h), [P, W], U8) for g in range(NR) for h in range(NG)}
+        imprec = {}
+        ys = kt("ys", [P, NR, G], U8)
+
+        xw_hbm = x_words.rearrange("g p n t -> p g (n t)")
+        hw_hbm = heat_words.rearrange("g p n -> p g n")
+        yw_hbm = out_1.rearrange("g p n t -> g p (n t)")
+
+        def scale_rows(eng, tile_ap, hbm, cols, qs=(0, 1, 2, 3)):
+            for q in qs:
+                eng.dma_start(out=tile_ap[32 * q:32 * q + 4, :, :].bitcast(I32),
+                              in_=hbm[:, 4 * q:4 * q + 4, cols].rearrange("g r n -> r g n").bitcast(I32))
+
+        def load_c(h, b):
+            nc.sync.dma_start(out=c_raw[h, b][:],
+                              in_=contacts[h * W:(h + 1) * W, b * W:(b + 1) * W].rearrange("(p t) n -> p t n", t=4))
+
+        def load_hw(g):
+            nc.sync.dma_start(out=hw[g][:].bitcast(I32), in_=hw_hbm[:, :, 2 * W * g:2 * W * (g + 1)].bitcast(I32))
+
+        nc.vector.memset(warm[:, 0:8], 0.0)
+        nc.vector.memset(hs0[:].bitcast(I32), 0)
+        nc.vector.memset(xs_raw[:].bitcast(I32), 0)
+        nc.scalar.activation(out=warm[:, 8:16], in_=warm[:, 0:8], func=ACT.Tanh)
+        nc.sync.dma_start(out=imp_col[:], in_=imports.rearrange("(n m) -> n m", m=8))
+        nc.sync.dma_start(out=rec_raw[:, :, 0:4], in_=recovery.rearrange("(g p s) -> p g s", p=P, s=4))
+        nc.sync.dma_start(out=xw_raw[0][:], in_=xw_hbm[:, :, 0:4 * W].bitcast(I32))
+        load_hw(0)
+        make_identity(nc, ident[:])
+        scale_rows(nc.gpsimd, hs0, heat_scales, slice(0, W), (2, 3))
+        scale_rows(nc.sync, xs_raw, x_scales, slice(0, G))
+        scale_rows(nc.sync, hs0, heat_scales, slice(0, W), (0, 1))
+        nc.sync.dma_start(out=xw_raw[1][:], in_=xw_hbm[:, :, 4 * W:8 * W].bitcast(I32))
+        nc.vector.memset(hs12[:].bitcast(I32), 0)
+        nc.vector.tensor_copy(out=rec[:], in_=rec_raw[:, :, 0:4])
+        load_c(0, 0)
+        nc.sync.dma_start(out=inf_raw[:, 0:NG, 0:4], in_=infectivity.rearrange("(h p t) -> p h t", p=P, t=4))
+        load_c(1, 0)
+        load_hw(1)
+        scale_rows(nc.sync, hs12, heat_scales, slice(W, R))
+        load_c(0, 1)
+        load_c(1, 1)
+        load_hw(2)
+
+        def spread_imports():
+            imp_ps = psum.tile([P, 8, P], BF16, name="imp_ps", tag="p", bufs=PB)
+            for m in range(8):
+                nc.tensor.transpose(imp_ps[:, m, :], imp_col[:, m:m + 1].to_broadcast([P, P]), ident[:])
+            nc.scalar.copy(out=imp_row[:].rearrange("p (n m) -> p n m", m=8), in_=imp_ps[:].rearrange("p m n -> p n m"))
+
+        inf_t = kt("inf_t", [P, P], BF16)
+        inf_bank = {}
+
+        def inf_turn():
+            t_ps = psum.tile([P, P], BF16, name="t_ps", tag="p", bufs=PB)
+            nc.tensor.transpose(t_ps[:], inf_raw[:].rearrange("p h t -> p (h t)"), ident[:])
+            nc.scalar.copy(out=inf_t[:], in_=t_ps[:])
+
+        def inf_back():
+            inf_bank[0] = psum.tile([P, 8, 16], BF16, name="inf_ps", tag="inf", bufs=1)
+            nc.tensor.transpose(inf_bank[0][:].rearrange("p h t -> p (h t)"), inf_t[:], ident[:])
+
+        def perm_words0(k):
+            nc.vector.tensor_copy(out=xw[0][:, k, :].rearrange("p (t m) -> p t m", t=4),
+                                  in_=xw_raw[0][:, k, :].rearrange("p (m t) -> p t m", t=4))
+
+        def perm_words1():
+            nc.vector.tensor_copy(out=xw[1][:].rearrange("p k (t m) -> p t k m", t=4),
+                                  in_=xw_raw[1][:].rearrange("p k (m t) -> p t k m", t=4))
+
+        def perm_scales0(k):
+            nc.vector.tensor_copy(out=xs[0][:, k, :].rearrange("p (t m) -> p t m", t=4),
+                                  in_=xs_raw[:, k, 0:W].rearrange("p (m t) -> p t m", t=4))
+
+        def perm_scales1():
+            nc.vector.tensor_copy(out=xs[1][:].rearrange("p k (t m) -> p t k m", t=4),
+                                  in_=xs_raw[:, :, W:G].rearrange("p k (m t) -> p t k m", t=4))
+
+        def make_imprec(eng, g, s, b=None):
+            if b is None:
+                both = flow.tile([P, G], F32, name="imprec2", bufs=12)
+                imprec[g, 0, s], imprec[g, 1, s] = both[:, 0:W], both[:, W:G]
+                dst, src = both[:], imp_row[:]
+            else:
+                one = flow.tile([P, W], F32, name="imprec", bufs=4)
+                imprec[g, b, s] = one[:]
+                dst, src = one[:], imp_row[:, b * W:(b + 1) * W]
+            if eng is nc.scalar:
+                nc.scalar.activation(out=dst, in_=src, func=ACT.Copy, scale=rec[:, g, s:s + 1])
+            elif eng is nc.vector:
+                nc.vector.tensor_scalar(out=dst, in0=src, scalar1=rec[:, g, s:s + 1], scalar2=None, op0=ALU.mult)
+            else:
+                nc.gpsimd.tensor_scalar(out=dst, in0=src, scalar1=rec[:, g, s:s + 1], scalar2=0.0,
+                                        op0=ALU.mult, op1=ALU.add)
+
+        def cti_out(t):
+            return t.rearrange("p (c i) t -> p c t i", i=4)
+
+        def cti_in(t):
+            return t.rearrange("p t (c i) -> p c t i", i=4)
+
+        c_bf = {(h, b): kt("c_bf%d%d" % (h, b), [P, W, 4], BF16) for h in range(NG) for b in range(NG)}
+
+        def quant(src, words, scales):
+            nc.vector.quantize_mx(out=words.bitcast(FP8X4), scales=scales, in_=src.rearrange("p n t -> p (n t)"))
+
+        def quant_c(h, b):
+            quant(c_bf[h, b][:], cw[h, b][:], cs[h, b][:])
+
+        d_ps = {}
+        th = {}
+        z_bf = {}
+
+        def h_scales(g, k):
+            return hs0[:, k, :] if g == 0 else hs12[:, k, (g - 1) * W:g * W]
+
+        def spread_pass(g, h, t, k):
+            if k == 0:
+                d_ps[g, h, t] = psum.tile([P, W], F32, name="d_ps", tag="d", bufs=DB)
+            cols = slice(t * P, (t + 1) * P)
+            nc.tensor.matmul_mx(out=d_ps[g, h, t][:], lhsT=xw[h][:, k, cols].bitcast(FP8X4), lhsT_scale=xs[h][:, k, cols],
+                                rhs=hw[g][:, k, :].bitcast(FP4X4), rhs_scale=h_scales(g, k),
+                                start=(k == 0), stop=(k == NR - 1))
+
+        def saturate(g, h, t):
+            if t == 0:
+                th[g, h] = flow.tile([P, 4, W], F32, name="th", bufs=3, align_bytes=64)
+            nc.scalar.activation(out=th[g, h][:, t, :].rearrange("p (s m) -> p s m", s=4),
+                                 in_=d_ps[g, h, t][:].rearrange("p (m s) -> p s m", s=4), func=ACT.Tanh)
+
+        def spread(g, h):
+            for t in range(4):
+                for k in range(NR):
+                    spread_pass(g, h, t, k)
+
+        def spread_first():
+            for t in range(4):
+                spread_pass(0, 0, t, 0)
+            for t in range(4):
+                spread_pass(0, 0, t, 1)
+                spread_pass(0, 0, t, 2)
+
+        def tanh(g, h, ts=(0, 1, 2, 3)):
+            for t in ts:
+                saturate(g, h, t)
+
+        def weigh(g, h, from_psum=False):
+            if from_psum:
+                fac = inf_bank[0][:, h, 0:4].unsqueeze(1).unsqueeze(3).to_broadcast([P, W // 4, 4, 4])
+            else:
+                fac = inf[:, h, :, :].unsqueeze(1).to_broadcast([P, W // 4, 4, 4])
+            z_bf[g, h] = flow.tile([P, W, 4], BF16, name="z_bf", bufs=2, align_bytes=64)
+            nc.vector.tensor_tensor(out=cti_out(z_bf[g, h][:]), in0=cti_in(th[g, h][:]),
+                                    in1=fac, op=ALU.mult)
+
+        def quant_z(g, h):
+            quant(z_bf[g, h][:], zw[g, h][:], zs[g, h][:])
+
+        y = {}
+        y_bf = {}
+
+        p_ps = {}
+
+        def contact(g, b):
+            for s in range(4):
+                p_ps[g, b, s] = psum.tile([P, W], F32, name="p_ps", tag="p", bufs=PB)
+                cols = slice(s * P, (s + 1) * P)
+                for h in range(NG):
+                    nc.tensor.matmul_mx(out=p_ps[g, b, s][:], lhsT=zw[g, h][:, cols].bitcast(FP8X4),
+                                        lhsT_scale=zs[g, h][:, cols],
+                                        rhs=cw[h, b][:].bitcast(FP8X4), rhs_scale=cs[h, b][:],
+                                        start=(h == 0), stop=(h == NG - 1))
+
+        def finish(g, b):
+            y[g, b] = flow.tile([P, 4, W], F32, name="y", bufs=3, align_bytes=64)
+            y_bf[g, b] = flow.tile([P, W, 4], BF16, name="y_bf", bufs=3, align_bytes=64)
+            rows = out_0[g * W:(g + 1) * W, b * W:(b + 1) * W].rearrange("(p s) n -> p s n", s=4)
+            for s in range(4):
+                nc.vector.scalar_tensor_tensor(out=y[g, b][:, s, :], in0=p_ps[g, b, s][:], scalar=rec[:, g, s:s + 1],
+                                               in1=imprec[g, b, s], op0=ALU.mult, op1=ALU.add)
+                nc.sync.dma_start(out=rows[:, s, :], in_=y[g, b][:, s, :])
+
+        def weave(eng, dst, src, lo, hi):
+            copy = nc.scalar.copy if eng is nc.scalar else nc.vector.tensor_copy
+            copy(out=cti_out(dst[:, lo:hi, :]), in_=cti_in(src[:, :, lo:hi]))
+
+        def weave_y(eng, g, b, lo=0, hi=W):
+            weave(eng, y_bf[g, b], y[g, b], lo, hi)
+
+        def weave_c(eng, h, b, lo=0, hi=W):
+            weave(eng, c_bf[h, b], c_raw[h, b], lo, hi)
+
+        def store_scales(gs):
+            for q in range(4):
+                nc.sync.dma_start(out=out_2[gs, 4 * q:4 * q + 4, :].rearrange("g r n -> r g n").bitcast(I32),
+                                  in_=ys[32 * q:32 * q + 4, gs, :].bitcast(I32))
+
+        def quant_y(g, b):
+            yw = flow.tile([P, W], I32, name="yw", bufs=3, align_bytes=64)
+            quant(y_bf[g, b][:], yw[:], ys[:, g, b * W:(b + 1) * W])
+            nc.sync.dma_start(out=yw_hbm[g, :, 4 * W * b:4 * W * (b + 1)].bitcast(I32), in_=yw[:])
+
+        S, V = nc.scalar, nc.vector
+
+        def small_casts():
+            nc.vector.tensor_copy(out=rec[:], in_=rec_raw[:, :, 0:4])
+            nc.vector.tensor_copy(out=inf[:], in_=inf_raw[:, 0:NG, 0:4].unsqueeze(3).to_broadcast([P, NG, 4, 4]))
+
+        H = W // 2
+        spread_imports()
+        for k in range(NR):
+            perm_words0(k)
+            perm_scales0(k)
+        spread_first()
+        perm_scales1()
+        make_imprec(S, 0, 0)
+        make_imprec(S, 0, 1)
+        make_imprec(S, 0, 2)
+        make_imprec(V, 2, 1)
+        perm_words1()
+        weave_c(V, 0, 0)
+        make_imprec(S, 0, 3)
+        tanh(0, 0)
+        spread(0, 1)
+        nc.vector.tensor_copy(out=inf[:], in_=inf_raw[:, 0:NG, 0:4].unsqueeze(3).to_broadcast([P, NG, 4, 4]))
+        weave_c(V, 1, 0)
+        weigh(0, 0)
+        quant_c(0, 0)
+        quant_c(1, 0)
+        quant_z(0, 0)
+        tanh(0, 1, (0, 1))
+        weave_c(S, 0, 1, 0, H)
+        tanh(0, 1, (2, 3))
+        spread(1, 0)
+        weave_c(S, 0, 1, H, W)
+        weigh(0, 1)
+        make_imprec(V, 2, 2)
+        quant_z(0, 1)
+        tanh(1, 0)
+        spread(1, 1)
+        contact(0, 0)
+        weigh(1, 0)
+        quant_c(0, 1)
+        quant_z(1, 0)
+        weave_c(S, 1, 1)
+        finish(0, 0)
+        quant_c(1, 1)
+        tanh(1, 1)
+        spread(2, 0)
+        contact(0, 1)
+        weigh(1, 1)
+        make_imprec(S, 1, 0)
+        make_imprec(S, 1, 1)
+        tanh(2, 0)
+        finish(0, 1)
+        quant_z(1, 1)
+        spread(2, 1)
+        contact(1, 0)
+        weave_y(S, 0, 0)
+        weigh(2, 0)
+        quant_y(0, 0)
+        quant_z(2, 0)
+        make_imprec(S, 1, 2)
+        make_imprec(S, 1, 3)
+        tanh(2, 1)
+        finish(1, 0)
+        contact(1, 1)
+        weave_y(S, 0, 1)
+        weigh(2, 1)
+        weave_y(S, 1, 0)
+        quant_y(0, 1)
+        store_scales(slice(0, 1))
+        quant_z(2, 1)
+        make_imprec(S, 2, 0)
+        make_imprec(S, 2, 3)
+        finish(1, 1)
+        contact(2, 0)
+        weave_y(S, 1, 1)
+        quant_y(1, 0)
+        finish(2, 0)
+        contact(2, 1)
+        weave_y(S, 2, 0)
+        quant_y(1, 1)
+        finish(2, 1)
+        quant_y(2, 0)
+        weave_y(V, 2, 1, 0, 320)
+        weave_y(S, 2, 1, 320, W)
+        quant_y(2, 1)
+        store_scales(slice(1, 3))

@@ -16,17 +16,19 @@ ACT = mybir.ActivationFunctionType
 ALU = mybir.AluOpType
 
 P = 128
-PB = 4
-DB = 4
 W = 512
 NR = R // W
 NG = G // W
+PB = 4
+DB = 4
+DTAG = "d"
 
 
 def tile_heat_contact_step_h2_kernel(tc, x_words, x_scales, heat_words, heat_scales,
                                                 infectivity, contacts, imports, recovery,
                                                 out_0, out_1, out_2):
     nc = tc.nc
+    S, V, GP = nc.scalar, nc.vector, nc.gpsimd
     with ExitStack() as ctx:
         keep = ctx.enter_context(tc.tile_pool(name="keep", bufs=1))
         flow = ctx.enter_context(tc.tile_pool(name="flow", bufs=2))
@@ -36,28 +38,36 @@ def tile_heat_contact_step_h2_kernel(tc, x_words, x_scales, heat_words, heat_sca
         def kt(name, shape, dt):
             return keep.tile(shape, dt, name=name, align_bytes=64)
 
-        ident = kt("ident", [P, P], BF16)
+        hb = [(h, b) for h in range(NG) for b in range(NG)]
+        gh = [(g, h) for g in range(NR) for h in range(NG)]
+        ident = kt("ident", [P, P], F32)
         warm = kt("warm", [P, 16], F32)
         imp_col = kt("imp_col", [P, 8], BF16)
         imp_row = kt("imp_row", [P, G], BF16)
         rec_raw = kt("rec_raw", [P, NR, 16], BF16)
         rec = kt("rec", [P, NR, 4], F32)
-        inf_raw = kt("inf_raw", [P, 8, 16], BF16)
-        inf = kt("inf", [P, NG, 4, 4], F32)
+        inf_raw = kt("inf_raw", [P, NG, 16], BF16)
+        inf_sq = kt("inf_sq", [P, P], F32)
+        inf_t = kt("inf_t", [P, P], F32)
         xs_raw = kt("xs_raw", [P, NR, G], U8)
         xs = [kt("xs%d" % h, [P, NR, W], U8) for h in range(NG)]
         xw_raw = [kt("xw_raw%d" % h, [P, NR, W], I32) for h in range(NG)]
         xw = [kt("xw%d" % h, [P, NR, W], I32) for h in range(NG)]
-        hw = [kt("hw%d" % g, [P, NR, 2 * W], U8) for g in range(NR)]
+        hw0 = kt("hw0", [P, NR, 2 * W], U8)
+        hw12 = kt("hw12", [P, NR, 4 * W], U8)
         hs0 = kt("hs0", [P, NR, W], U8)
         hs12 = kt("hs12", [P, NR, 2 * W], U8)
-        c_raw = {(h, b): kt("c_raw%d%d" % (h, b), [P, 4, W], BF16) for h in range(NG) for b in range(NG)}
-        cw = {(h, b): kt("cw%d%d" % (h, b), [P, W], I32) for h in range(NG) for b in range(NG)}
-        cs = {(h, b): kt("cs%d%d" % (h, b), [P, W], U8) for h in range(NG) for b in range(NG)}
-        zw = {(g, h): kt("zw%d%d" % (g, h), [P, W], I32) for g in range(NR) for h in range(NG)}
-        zs = {(g, h): kt("zs%d%d" % (g, h), [P, W], U8) for g in range(NR) for h in range(NG)}
-        imprec = {}
+        c_raw = [kt("c_raw%d" % h, [P, 4, G], BF16) for h in range(NG)]
+        c_bf = {k: kt("c_bf%d%d" % k, [P, W, 4], BF16) for k in hb}
+        cw = {k: kt("cw%d%d" % k, [P, W], I32) for k in hb}
+        cs = {k: kt("cs%d%d" % k, [P, W], U8) for k in hb}
+        zw = {k: kt("zw%d%d" % k, [P, W], I32) for k in gh}
+        zs = {k: kt("zs%d%d" % k, [P, W], U8) for k in gh}
+        idle_bf = kt("idle_bf", [P, 4 * P], BF16)
+        idle_w = kt("idle_w", [P, P], I32)
+        idle_s = kt("idle_s", [P, P], U8)
         ys = kt("ys", [P, NR, G], U8)
+        imprec, inf_bank, d_ps, th, z_bf, z_flat, p_ps, y, y_bf = {}, {}, {}, {}, {}, {}, {}, {}, {}
 
         xw_hbm = x_words.rearrange("g p n t -> p g (n t)")
         hw_hbm = heat_words.rearrange("g p n -> p g n")
@@ -68,70 +78,55 @@ def tile_heat_contact_step_h2_kernel(tc, x_words, x_scales, heat_words, heat_sca
                 eng.dma_start(out=tile_ap[32 * q:32 * q + 4, :, :].bitcast(I32),
                               in_=hbm[:, 4 * q:4 * q + 4, cols].rearrange("g r n -> r g n").bitcast(I32))
 
-        def load_c(h, b):
-            nc.sync.dma_start(out=c_raw[h, b][:],
-                              in_=contacts[h * W:(h + 1) * W, b * W:(b + 1) * W].rearrange("(p t) n -> p t n", t=4))
+        def load_x(h):
+            nc.sync.dma_start(out=xw_raw[h][:], in_=xw_hbm[:, :, 4 * W * h:4 * W * (h + 1)].bitcast(I32))
 
-        def load_hw(g):
-            nc.sync.dma_start(out=hw[g][:].bitcast(I32), in_=hw_hbm[:, :, 2 * W * g:2 * W * (g + 1)].bitcast(I32))
+        def load_c(h):
+            nc.sync.dma_start(out=c_raw[h][:], in_=contacts[h * W:(h + 1) * W, :].rearrange("(p t) n -> p t n", t=4))
 
-        nc.vector.memset(warm[:, 0:8], 0.0)
-        nc.vector.memset(hs0[:].bitcast(I32), 0)
-        nc.vector.memset(xs_raw[:].bitcast(I32), 0)
-        nc.scalar.activation(out=warm[:, 8:16], in_=warm[:, 0:8], func=ACT.Tanh)
-        nc.sync.dma_start(out=imp_col[:], in_=imports.rearrange("(n m) -> n m", m=8))
-        nc.sync.dma_start(out=rec_raw[:, :, 0:4], in_=recovery.rearrange("(g p s) -> p g s", p=P, s=4))
-        nc.sync.dma_start(out=xw_raw[0][:], in_=xw_hbm[:, :, 0:4 * W].bitcast(I32))
-        load_hw(0)
-        make_identity(nc, ident[:])
-        scale_rows(nc.gpsimd, hs0, heat_scales, slice(0, W), (2, 3))
-        scale_rows(nc.sync, xs_raw, x_scales, slice(0, G))
-        scale_rows(nc.sync, hs0, heat_scales, slice(0, W), (0, 1))
-        nc.sync.dma_start(out=xw_raw[1][:], in_=xw_hbm[:, :, 4 * W:8 * W].bitcast(I32))
-        nc.vector.memset(hs12[:].bitcast(I32), 0)
-        nc.vector.tensor_copy(out=rec[:], in_=rec_raw[:, :, 0:4])
-        load_c(0, 0)
-        nc.sync.dma_start(out=inf_raw[:, 0:NG, 0:4], in_=infectivity.rearrange("(h p t) -> p h t", p=P, t=4))
-        load_c(1, 0)
-        load_hw(1)
-        scale_rows(nc.sync, hs12, heat_scales, slice(W, R))
-        load_c(0, 1)
-        load_c(1, 1)
-        load_hw(2)
+        def load_hw(dst, lo, hi):
+            nc.sync.dma_start(out=dst[:].bitcast(I32), in_=hw_hbm[:, :, 2 * W * lo:2 * W * hi].bitcast(I32))
+
+        def h_words(g, k):
+            return hw0[:, k, :] if g == 0 else hw12[:, k, (g - 1) * 2 * W:g * 2 * W]
 
         def spread_imports():
-            imp_ps = psum.tile([P, 8, P], BF16, name="imp_ps", tag="p", bufs=PB)
-            for m in range(8):
-                nc.tensor.transpose(imp_ps[:, m, :], imp_col[:, m:m + 1].to_broadcast([P, P]), ident[:])
-            nc.scalar.copy(out=imp_row[:].rearrange("p (n m) -> p n m", m=8), in_=imp_ps[:].rearrange("p m n -> p n m"))
+            imp_ps = psum.tile([P, 4, P], F32, name="imp_ps", tag="p", bufs=PB)
+            for m in range(4):
+                nc.tensor.transpose(imp_ps[:, m, :], imp_col[:].bitcast(F32)[:, m:m + 1].to_broadcast([P, P]), ident[:])
+            nc.scalar.copy(out=imp_row[:].bitcast(F32).rearrange("p (n m) -> p n m", m=4),
+                           in_=imp_ps[:].rearrange("p m n -> p n m"))
 
-        inf_t = kt("inf_t", [P, P], BF16)
-        inf_bank = {}
+        def warm_tensor(n):
+            idle_ps = psum.tile([P, P], F32, name="idle_ps", tag="p", bufs=PB)
+            for i in range(n):
+                nc.tensor.matmul_mx(out=idle_ps[:], lhsT=idle_w[:].bitcast(FP8X4), lhsT_scale=idle_s[:],
+                                    rhs=idle_w[:].bitcast(FP8X4), rhs_scale=idle_s[:], start=True, stop=True)
 
-        def inf_turn():
-            t_ps = psum.tile([P, P], BF16, name="t_ps", tag="p", bufs=PB)
-            nc.tensor.transpose(t_ps[:], inf_raw[:].rearrange("p h t -> p (h t)"), ident[:])
-            nc.scalar.copy(out=inf_t[:], in_=t_ps[:])
+        def inf_cast():
+            nc.vector.tensor_copy(out=inf_sq[:, 0:32].rearrange("p (h t i) -> p h t i", t=4, i=4),
+                                  in_=inf_raw[:, :, 0:4].unsqueeze(3).to_broadcast([P, NG, 4, 4]))
+
+        def inf_turn_pe():
+            inf_bank[1] = psum.tile([P, P], F32, name="t_ps", tag="p", bufs=PB)
+            nc.tensor.transpose(inf_bank[1][:], inf_sq[:], ident[:])
+
+        def inf_turn_copy():
+            nc.scalar.copy(out=inf_t[:], in_=inf_bank[1][:])
 
         def inf_back():
-            inf_bank[0] = psum.tile([P, 8, 16], BF16, name="inf_ps", tag="inf", bufs=1)
-            nc.tensor.transpose(inf_bank[0][:].rearrange("p h t -> p (h t)"), inf_t[:], ident[:])
+            inf_bank[0] = psum.tile([P, P], F32, name="inf_ps", tag="inf", bufs=1)
+            nc.tensor.transpose(inf_bank[0][:], inf_t[:], ident[:])
 
-        def perm_words0(k):
-            nc.vector.tensor_copy(out=xw[0][:, k, :].rearrange("p (t m) -> p t m", t=4),
-                                  in_=xw_raw[0][:, k, :].rearrange("p (m t) -> p t m", t=4))
+        def perm(dst, src):
+            nc.vector.tensor_copy(out=dst.rearrange("p k (t m) -> p t k m", t=4),
+                                  in_=src.rearrange("p k (m t) -> p t k m", t=4))
 
-        def perm_words1():
-            nc.vector.tensor_copy(out=xw[1][:].rearrange("p k (t m) -> p t k m", t=4),
-                                  in_=xw_raw[1][:].rearrange("p k (m t) -> p t k m", t=4))
+        def perm_words(h, k0=0, k1=NR):
+            perm(xw[h][:, k0:k1, :], xw_raw[h][:, k0:k1, :])
 
-        def perm_scales0(k):
-            nc.vector.tensor_copy(out=xs[0][:, k, :].rearrange("p (t m) -> p t m", t=4),
-                                  in_=xs_raw[:, k, 0:W].rearrange("p (m t) -> p t m", t=4))
-
-        def perm_scales1():
-            nc.vector.tensor_copy(out=xs[1][:].rearrange("p k (t m) -> p t k m", t=4),
-                                  in_=xs_raw[:, :, W:G].rearrange("p k (m t) -> p t k m", t=4))
+        def perm_scales(h, k0=0, k1=NR):
+            perm(xs[h][:, k0:k1, :], xs_raw[:, k0:k1, h * W:(h + 1) * W])
 
         def make_imprec(eng, g, s, b=None):
             if b is None:
@@ -139,12 +134,12 @@ def tile_heat_contact_step_h2_kernel(tc, x_words, x_scales, heat_words, heat_sca
                 imprec[g, 0, s], imprec[g, 1, s] = both[:, 0:W], both[:, W:G]
                 dst, src = both[:], imp_row[:]
             else:
-                one = flow.tile([P, W], F32, name="imprec", bufs=4)
+                one = flow.tile([P, W], F32, name="imprec", bufs=1)
                 imprec[g, b, s] = one[:]
                 dst, src = one[:], imp_row[:, b * W:(b + 1) * W]
-            if eng is nc.scalar:
+            if eng is S:
                 nc.scalar.activation(out=dst, in_=src, func=ACT.Copy, scale=rec[:, g, s:s + 1])
-            elif eng is nc.vector:
+            elif eng is V:
                 nc.vector.tensor_scalar(out=dst, in0=src, scalar1=rec[:, g, s:s + 1], scalar2=None, op0=ALU.mult)
             else:
                 nc.gpsimd.tensor_scalar(out=dst, in0=src, scalar1=rec[:, g, s:s + 1], scalar2=0.0,
@@ -156,7 +151,19 @@ def tile_heat_contact_step_h2_kernel(tc, x_words, x_scales, heat_words, heat_sca
         def cti_in(t):
             return t.rearrange("p t (c i) -> p c t i", i=4)
 
-        c_bf = {(h, b): kt("c_bf%d%d" % (h, b), [P, W, 4], BF16) for h in range(NG) for b in range(NG)}
+        def weave(eng, dst, src, lo, hi):
+            if eng is GP:
+                nc.gpsimd.tensor_scalar(out=cti_out(dst[:, lo:hi, :]), in0=cti_in(src[:, :, lo:hi]),
+                                        scalar1=1.0, scalar2=0.0, op0=ALU.mult, op1=ALU.add)
+            else:
+                copy = nc.scalar.copy if eng is S else nc.vector.tensor_copy
+                copy(out=cti_out(dst[:, lo:hi, :]), in_=cti_in(src[:, :, lo:hi]))
+
+        def weave_y(eng, g, b, lo=0, hi=W):
+            weave(eng, y_bf[g, b], y[g, b], lo, hi)
+
+        def weave_c(eng, h, b, lo=0, hi=W):
+            weave(eng, c_bf[h, b], c_raw[h][:, :, b * W:(b + 1) * W], lo, hi)
 
         def quant(src, words, scales):
             nc.vector.quantize_mx(out=words.bitcast(FP8X4), scales=scales, in_=src.rearrange("p n t -> p (n t)"))
@@ -164,29 +171,19 @@ def tile_heat_contact_step_h2_kernel(tc, x_words, x_scales, heat_words, heat_sca
         def quant_c(h, b):
             quant(c_bf[h, b][:], cw[h, b][:], cs[h, b][:])
 
-        d_ps = {}
-        th = {}
-        z_bf = {}
-
         def h_scales(g, k):
             return hs0[:, k, :] if g == 0 else hs12[:, k, (g - 1) * W:g * W]
 
         def spread_pass(g, h, t, k):
             if k == 0:
-                d_ps[g, h, t] = psum.tile([P, W], F32, name="d_ps", tag="d", bufs=DB)
+                d_ps[g, h, t] = psum.tile([P, W], F32, name="d_ps", tag=DTAG, bufs=DB)
             cols = slice(t * P, (t + 1) * P)
             nc.tensor.matmul_mx(out=d_ps[g, h, t][:], lhsT=xw[h][:, k, cols].bitcast(FP8X4), lhsT_scale=xs[h][:, k, cols],
-                                rhs=hw[g][:, k, :].bitcast(FP4X4), rhs_scale=h_scales(g, k),
+                                rhs=h_words(g, k).bitcast(FP4X4), rhs_scale=h_scales(g, k),
                                 start=(k == 0), stop=(k == NR - 1))
 
-        def saturate(g, h, t):
-            if t == 0:
-                th[g, h] = flow.tile([P, 4, W], F32, name="th", bufs=3, align_bytes=64)
-            nc.scalar.activation(out=th[g, h][:, t, :].rearrange("p (s m) -> p s m", s=4),
-                                 in_=d_ps[g, h, t][:].rearrange("p (m s) -> p s m", s=4), func=ACT.Tanh)
-
-        def spread(g, h):
-            for t in range(4):
+        def spread(g, h, ts=(0, 1, 2, 3)):
+            for t in ts:
                 for k in range(NR):
                     spread_pass(g, h, t, k)
 
@@ -199,27 +196,23 @@ def tile_heat_contact_step_h2_kernel(tc, x_words, x_scales, heat_words, heat_sca
 
         def tanh(g, h, ts=(0, 1, 2, 3)):
             for t in ts:
-                saturate(g, h, t)
+                if t == 0:
+                    th[g, h] = flow.tile([P, 4, W], F32, name="th", bufs=3, align_bytes=64)
+                nc.scalar.activation(out=th[g, h][:, t, :].rearrange("p (s m) -> p s m", s=4),
+                                     in_=d_ps[g, h, t][:].rearrange("p (m s) -> p s m", s=4), func=ACT.Tanh)
 
         def weigh(g, h, from_psum=False):
-            if from_psum:
-                fac = inf_bank[0][:, h, 0:4].unsqueeze(1).unsqueeze(3).to_broadcast([P, W // 4, 4, 4])
-            else:
-                fac = inf[:, h, :, :].unsqueeze(1).to_broadcast([P, W // 4, 4, 4])
+            src = inf_bank[0] if from_psum else inf_sq
+            fac = src[:, 16 * h:16 * h + 16].rearrange("p (t i) -> p t i", i=4).unsqueeze(1)
             z_bf[g, h] = flow.tile([P, W, 4], BF16, name="z_bf", bufs=2, align_bytes=64)
             nc.vector.tensor_tensor(out=cti_out(z_bf[g, h][:]), in0=cti_in(th[g, h][:]),
-                                    in1=fac, op=ALU.mult)
+                                    in1=fac.to_broadcast([P, W // 4, 4, 4]), op=ALU.mult)
 
         def quant_z(g, h):
             quant(z_bf[g, h][:], zw[g, h][:], zs[g, h][:])
 
-        y = {}
-        y_bf = {}
-
-        p_ps = {}
-
-        def contact(g, b):
-            for s in range(4):
+        def contact(g, b, ss=(0, 1, 2, 3)):
+            for s in ss:
                 p_ps[g, b, s] = psum.tile([P, W], F32, name="p_ps", tag="p", bufs=PB)
                 cols = slice(s * P, (s + 1) * P)
                 for h in range(NG):
@@ -228,7 +221,7 @@ def tile_heat_contact_step_h2_kernel(tc, x_words, x_scales, heat_words, heat_sca
                                         rhs=cw[h, b][:].bitcast(FP8X4), rhs_scale=cs[h, b][:],
                                         start=(h == 0), stop=(h == NG - 1))
 
-        def finish(g, b):
+        def finish(g, b, then=None):
             y[g, b] = flow.tile([P, 4, W], F32, name="y", bufs=3, align_bytes=64)
             y_bf[g, b] = flow.tile([P, W, 4], BF16, name="y_bf", bufs=3, align_bytes=64)
             rows = out_0[g * W:(g + 1) * W, b * W:(b + 1) * W].rearrange("(p s) n -> p s n", s=4)
@@ -236,16 +229,8 @@ def tile_heat_contact_step_h2_kernel(tc, x_words, x_scales, heat_words, heat_sca
                 nc.vector.scalar_tensor_tensor(out=y[g, b][:, s, :], in0=p_ps[g, b, s][:], scalar=rec[:, g, s:s + 1],
                                                in1=imprec[g, b, s], op0=ALU.mult, op1=ALU.add)
                 nc.sync.dma_start(out=rows[:, s, :], in_=y[g, b][:, s, :])
-
-        def weave(eng, dst, src, lo, hi):
-            copy = nc.scalar.copy if eng is nc.scalar else nc.vector.tensor_copy
-            copy(out=cti_out(dst[:, lo:hi, :]), in_=cti_in(src[:, :, lo:hi]))
-
-        def weave_y(eng, g, b, lo=0, hi=W):
-            weave(eng, y_bf[g, b], y[g, b], lo, hi)
-
-        def weave_c(eng, h, b, lo=0, hi=W):
-            weave(eng, c_bf[h, b], c_raw[h, b], lo, hi)
+                if then is not None:
+                    make_imprec(GP, then[0], s, then[1])
 
         def store_scales(gs):
             for q in range(4):
@@ -257,57 +242,78 @@ def tile_heat_contact_step_h2_kernel(tc, x_words, x_scales, heat_words, heat_sca
             quant(y_bf[g, b][:], yw[:], ys[:, g, b * W:(b + 1) * W])
             nc.sync.dma_start(out=yw_hbm[g, :, 4 * W * b:4 * W * (b + 1)].bitcast(I32), in_=yw[:])
 
-        S, V = nc.scalar, nc.vector
-
-        def small_casts():
-            nc.vector.tensor_copy(out=rec[:], in_=rec_raw[:, :, 0:4])
-            nc.vector.tensor_copy(out=inf[:], in_=inf_raw[:, 0:NG, 0:4].unsqueeze(3).to_broadcast([P, NG, 4, 4]))
+        nc.vector.memset(warm[:, 0:8], 0.0)
+        nc.vector.memset(hs0[:].bitcast(I32), 0)
+        nc.vector.memset(xs_raw[:].bitcast(I32), 0)
+        nc.scalar.activation(out=warm[:, 8:16], in_=warm[:, 0:8], func=ACT.Tanh)
+        nc.sync.dma_start(out=imp_col[:], in_=imports.rearrange("(n m) -> n m", m=8))
+        nc.sync.dma_start(out=rec_raw[:, :, 0:4], in_=recovery.rearrange("(g p s) -> p g s", p=P, s=4))
+        load_x(0)
+        load_hw(hw0, 0, 1)
+        make_identity(nc, ident[:])
+        scale_rows(nc.gpsimd, hs0, heat_scales, slice(0, W), (2, 3))
+        scale_rows(nc.sync, xs_raw, x_scales, slice(0, G))
+        scale_rows(nc.sync, hs0, heat_scales, slice(0, W), (0, 1))
+        load_x(1)
+        nc.vector.memset(idle_bf[:].bitcast(I32), 0)
+        nc.vector.quantize_mx(out=idle_w[:].bitcast(FP8X4), scales=idle_s[:], in_=idle_bf[:])
+        nc.vector.memset(hs12[:].bitcast(I32), 0)
+        nc.vector.tensor_copy(out=rec[:], in_=rec_raw[:, :, 0:4])
+        nc.sync.dma_start(out=inf_raw[:, :, 0:4], in_=infectivity.rearrange("(h p t) -> p h t", p=P, t=4))
+        load_c(0)
+        scale_rows(nc.sync, hs12, heat_scales, slice(W, R))
+        load_hw(hw12, 1, 3)
+        load_c(1)
 
         H = W // 2
         spread_imports()
+        warm_tensor(18)
         for k in range(NR):
-            perm_words0(k)
-            perm_scales0(k)
-        spread_first()
-        perm_scales1()
-        make_imprec(S, 0, 0)
-        make_imprec(S, 0, 1)
-        make_imprec(S, 0, 2)
+            perm_words(0, k, k + 1)
+        for k in range(NR):
+            perm_scales(0, k, k + 1)
+        spread(0, 0)
+        perm_scales(1)
+        for s in range(3):
+            make_imprec(S, 0, s)
         make_imprec(V, 2, 1)
-        perm_words1()
-        weave_c(V, 0, 0)
-        make_imprec(S, 0, 3)
+        perm_words(1)
+        inf_cast()
+        make_imprec(V, 0, 3)
         tanh(0, 0)
         spread(0, 1)
-        nc.vector.tensor_copy(out=inf[:], in_=inf_raw[:, 0:NG, 0:4].unsqueeze(3).to_broadcast([P, NG, 4, 4]))
-        weave_c(V, 1, 0)
         weigh(0, 0)
-        quant_c(0, 0)
-        quant_c(1, 0)
+        weave_c(V, 0, 0)
         quant_z(0, 0)
+        quant_c(0, 0)
         tanh(0, 1, (0, 1))
         weave_c(S, 0, 1, 0, H)
         tanh(0, 1, (2, 3))
-        spread(1, 0)
         weave_c(S, 0, 1, H, W)
+        spread(1, 0)
         weigh(0, 1)
-        make_imprec(V, 2, 2)
+        weave_c(V, 1, 0)
         quant_z(0, 1)
-        tanh(1, 0)
+        quant_c(1, 0)
+        tanh(1, 0, (0, 1))
+        weave_c(S, 1, 1, 0, H)
+        tanh(1, 0, (2, 3))
         spread(1, 1)
         contact(0, 0)
         weigh(1, 0)
         quant_c(0, 1)
         quant_z(1, 0)
-        weave_c(S, 1, 1)
+        weave_c(S, 1, 1, H, W)
+        make_imprec(S, 1, 0)
+        make_imprec(S, 1, 1)
         finish(0, 0)
         quant_c(1, 1)
         tanh(1, 1)
         spread(2, 0)
         contact(0, 1)
         weigh(1, 1)
-        make_imprec(S, 1, 0)
-        make_imprec(S, 1, 1)
+        make_imprec(S, 1, 2)
+        make_imprec(S, 1, 3)
         tanh(2, 0)
         finish(0, 1)
         quant_z(1, 1)
@@ -317,18 +323,17 @@ def tile_heat_contact_step_h2_kernel(tc, x_words, x_scales, heat_words, heat_sca
         weigh(2, 0)
         quant_y(0, 0)
         quant_z(2, 0)
-        make_imprec(S, 1, 2)
-        make_imprec(S, 1, 3)
+        weave_y(S, 0, 1)
         tanh(2, 1)
         finish(1, 0)
         contact(1, 1)
-        weave_y(S, 0, 1)
+        make_imprec(S, 2, 0)
         weigh(2, 1)
         weave_y(S, 1, 0)
         quant_y(0, 1)
         store_scales(slice(0, 1))
         quant_z(2, 1)
-        make_imprec(S, 2, 0)
+        make_imprec(S, 2, 2)
         make_imprec(S, 2, 3)
         finish(1, 1)
         contact(2, 0)

@@ -104,8 +104,8 @@ def tile_heat_contact_step_h2_kernel(tc, x_words, x_scales, heat_words, heat_sca
                                     rhs=idle_w[:].bitcast(FP8X4), rhs_scale=idle_s[:], start=True, stop=True)
 
         def inf_cast():
-            nc.vector.tensor_copy(out=inf_sq[:, 0:32].rearrange("p (h t i) -> p h t i", t=4, i=4),
-                                  in_=inf_raw[:, :, 0:4].unsqueeze(3).to_broadcast([P, NG, 4, 4]))
+            nc.vector.tensor_copy(out=inf_sq[:, 0:16].rearrange("p (h t i) -> p h t i", t=4, i=2),
+                                  in_=inf_raw[:, :, 0:4].unsqueeze(3).to_broadcast([P, NG, 4, 2]))
 
         def inf_turn_pe():
             inf_bank[1] = psum.tile([P, P], F32, name="t_ps", tag="p", bufs=PB)
@@ -123,7 +123,9 @@ def tile_heat_contact_step_h2_kernel(tc, x_words, x_scales, heat_words, heat_sca
                                   in_=src.rearrange("p k (m t) -> p t k m", t=4))
 
         def perm_words(h, k0=0, k1=NR):
-            perm(xw[h][:, k0:k1, :], xw_raw[h][:, k0:k1, :])
+            for k in range(k0, k1):
+                nc.vector.tensor_copy(out=xw[h][:, k, :].rearrange("p (u e m) -> p u m e", u=2, e=2),
+                                      in_=xw_raw[h][:, k, :].rearrange("p (m u e) -> p u m e", u=2, e=2))
 
         def perm_scales(h, k0=0, k1=NR):
             perm(xs[h][:, k0:k1, :], xs_raw[:, k0:k1, h * W:(h + 1) * W])
@@ -145,25 +147,25 @@ def tile_heat_contact_step_h2_kernel(tc, x_words, x_scales, heat_words, heat_sca
                 nc.gpsimd.tensor_scalar(out=dst, in0=src, scalar1=rec[:, g, s:s + 1], scalar2=0.0,
                                         op0=ALU.mult, op1=ALU.add)
 
-        def cti_out(t):
-            return t.rearrange("p (c i) t -> p c t i", i=4)
+        def cti_out(t, run):
+            return t.rearrange("p (c i) t -> p c t i", i=run)
 
-        def cti_in(t):
-            return t.rearrange("p t (c i) -> p c t i", i=4)
+        def cti_in(t, run):
+            return t.rearrange("p t (c i) -> p c t i", i=run)
 
-        def weave(eng, dst, src, lo, hi):
+        def weave(eng, dst, src, lo, hi, run):
             if eng is GP:
-                nc.gpsimd.tensor_scalar(out=cti_out(dst[:, lo:hi, :]), in0=cti_in(src[:, :, lo:hi]),
+                nc.gpsimd.tensor_scalar(out=cti_out(dst[:, lo:hi, :], run), in0=cti_in(src[:, :, lo:hi], run),
                                         scalar1=1.0, scalar2=0.0, op0=ALU.mult, op1=ALU.add)
             else:
                 copy = nc.scalar.copy if eng is S else nc.vector.tensor_copy
-                copy(out=cti_out(dst[:, lo:hi, :]), in_=cti_in(src[:, :, lo:hi]))
+                copy(out=cti_out(dst[:, lo:hi, :], run), in_=cti_in(src[:, :, lo:hi], run))
 
         def weave_y(eng, g, b, lo=0, hi=W):
-            weave(eng, y_bf[g, b], y[g, b], lo, hi)
+            weave(eng, y_bf[g, b], y[g, b], lo, hi, 2)
 
         def weave_c(eng, h, b, lo=0, hi=W):
-            weave(eng, c_bf[h, b], c_raw[h][:, :, b * W:(b + 1) * W], lo, hi)
+            weave(eng, c_bf[h, b], c_raw[h][:, :, b * W:(b + 1) * W], lo, hi, 4)
 
         def quant(src, words, scales):
             nc.vector.quantize_mx(out=words.bitcast(FP8X4), scales=scales, in_=src.rearrange("p n t -> p (n t)"))
@@ -203,10 +205,10 @@ def tile_heat_contact_step_h2_kernel(tc, x_words, x_scales, heat_words, heat_sca
 
         def weigh(g, h, from_psum=False):
             src = inf_bank[0] if from_psum else inf_sq
-            fac = src[:, 16 * h:16 * h + 16].rearrange("p (t i) -> p t i", i=4).unsqueeze(1)
+            fac = src[:, 8 * h:8 * h + 8].rearrange("p (t i) -> p t i", i=2).unsqueeze(1)
             z_bf[g, h] = flow.tile([P, W, 4], BF16, name="z_bf", bufs=2, align_bytes=64)
-            nc.vector.tensor_tensor(out=cti_out(z_bf[g, h][:]), in0=cti_in(th[g, h][:]),
-                                    in1=fac.to_broadcast([P, W // 4, 4, 4]), op=ALU.mult)
+            nc.vector.tensor_tensor(out=cti_out(z_bf[g, h][:], 2), in0=cti_in(th[g, h][:], 2),
+                                    in1=fac.to_broadcast([P, W // 2, 4, 2]), op=ALU.mult)
 
         def quant_z(g, h):
             quant(z_bf[g, h][:], zw[g, h][:], zs[g, h][:])

@@ -28,7 +28,7 @@ def tile_heat_contact_step_h2_kernel(tc, x_words, x_scales, heat_words, heat_sca
                                                 infectivity, contacts, imports, recovery,
                                                 out_0, out_1, out_2):
     nc = tc.nc
-    S, V, GP = nc.scalar, nc.vector, nc.gpsimd
+    S, V = nc.scalar, nc.vector
     with ExitStack() as ctx:
         keep = ctx.enter_context(tc.tile_pool(name="keep", bufs=1))
         flow = ctx.enter_context(tc.tile_pool(name="flow", bufs=2))
@@ -38,36 +38,36 @@ def tile_heat_contact_step_h2_kernel(tc, x_words, x_scales, heat_words, heat_sca
         def kt(name, shape, dt):
             return keep.tile(shape, dt, name=name, align_bytes=64)
 
-        hb = [(h, b) for h in range(NG) for b in range(NG)]
-        gh = [(g, h) for g in range(NR) for h in range(NG)]
         ident = kt("ident", [P, P], F32)
         warm = kt("warm", [P, 16], F32)
         imp_col = kt("imp_col", [P, 8], BF16)
         imp_row = kt("imp_row", [P, G], BF16)
         rec_raw = kt("rec_raw", [P, NR, 16], BF16)
         rec = kt("rec", [P, NR, 4], F32)
-        inf_raw = kt("inf_raw", [P, NG, 16], BF16)
+        inf_rows = kt("inf_rows", [P, P], BF16)
         inf_sq = kt("inf_sq", [P, P], F32)
-        inf_t = kt("inf_t", [P, P], F32)
+        inf = kt("inf", [P, 4 * NG, 2], F32)
         xs_raw = kt("xs_raw", [P, NR, G], U8)
-        xs = [kt("xs%d" % h, [P, NR, W], U8) for h in range(NG)]
-        xw_raw = [kt("xw_raw%d" % h, [P, NR, W], I32) for h in range(NG)]
-        xw = [kt("xw%d" % h, [P, NR, W], I32) for h in range(NG)]
-        hw0 = kt("hw0", [P, NR, 2 * W], U8)
-        hw12 = kt("hw12", [P, NR, 4 * W], U8)
         hs0 = kt("hs0", [P, NR, W], U8)
+        xs = [kt("xs%d" % h, [P, 4, NR, P], U8) for h in range(NG)]
+        xw_raw = [flow.tile([P, NR, W], I32, name="xw_raw%d" % h, tag="y", bufs=4, align_bytes=64) for h in range(NG)]
+        xw = [kt("xw%d" % h, [P, 4, NR, P], I32) for h in range(NG)]
+        hw = [kt("hw%d" % g, [P, NR, 2 * W], U8) for g in range(NR)]
         hs12 = kt("hs12", [P, NR, 2 * W], U8)
-        c_raw = [kt("c_raw%d" % h, [P, 4, G], BF16) for h in range(NG)]
-        c_bf = {k: kt("c_bf%d%d" % k, [P, W, 4], BF16) for k in hb}
-        cw = {k: kt("cw%d%d" % k, [P, W], I32) for k in hb}
-        cs = {k: kt("cs%d%d" % k, [P, W], U8) for k in hb}
-        zw = {k: kt("zw%d%d" % k, [P, W], I32) for k in gh}
-        zs = {k: kt("zs%d%d" % k, [P, W], U8) for k in gh}
+        c_raw = [flow.tile([P, 4, G], BF16, name="c_raw%d" % h, tag="y_bf", bufs=2, align_bytes=64) for h in range(NG)]
+        c_bf = [kt("c_bf%d" % b, [P, NG, W, 4], BF16) for b in range(NG)]
+        cw = [kt("cw%d" % b, [P, NG * W], I32) for b in range(NG)]
+        cs = [kt("cs%d" % b, [P, NG * W], U8) for b in range(NG)]
+        zw = [kt("zw%d" % g, [P, NG * W], I32) for g in range(NR)]
+        zs = [kt("zs%d" % g, [P, NG * W], U8) for g in range(NR)]
+        yw = [kt("yw%d" % g, [P, G], I32) for g in range(NR)]
+        imprec = [kt("imprec%d" % g, [P, 4, G], F32) for g in range(NR)]
+        z_rows = kt("z_rows", [P, 4, W], BF16)
         idle_bf = kt("idle_bf", [P, 4 * P], BF16)
         idle_w = kt("idle_w", [P, P], I32)
         idle_s = kt("idle_s", [P, P], U8)
         ys = kt("ys", [P, NR, G], U8)
-        imprec, inf_bank, d_ps, th, z_bf, z_flat, p_ps, y, y_bf = {}, {}, {}, {}, {}, {}, {}, {}, {}
+        inf_bank, d_ps, th, z_bf, p_ps, y, y_bf = {}, {}, {}, {}, {}, {}, {}
 
         xw_hbm = x_words.rearrange("g p n t -> p g (n t)")
         hw_hbm = heat_words.rearrange("g p n -> p g n")
@@ -81,14 +81,18 @@ def tile_heat_contact_step_h2_kernel(tc, x_words, x_scales, heat_words, heat_sca
         def load_x(h):
             nc.sync.dma_start(out=xw_raw[h][:], in_=xw_hbm[:, :, 4 * W * h:4 * W * (h + 1)].bitcast(I32))
 
-        def load_c(h):
-            nc.sync.dma_start(out=c_raw[h][:], in_=contacts[h * W:(h + 1) * W, :].rearrange("(p t) n -> p t n", t=4))
+        def load_c(h, lo=0, hi=G):
+            rows = contacts[h * W:(h + 1) * W, :].rearrange("(u t r) n -> r u t n", t=4, r=4)
+            for r in range(4):
+                nc.sync.dma_start(out=c_raw[h][r:P:4, :, lo:hi], in_=rows[r][:, :, lo:hi])
 
-        def load_hw(dst, lo, hi):
-            nc.sync.dma_start(out=dst[:].bitcast(I32), in_=hw_hbm[:, :, 2 * W * lo:2 * W * hi].bitcast(I32))
+        def load_inf(eng):
+            rows = infectivity.rearrange("(h u t r) -> h t u r", h=NG, t=4, r=4)
+            for h in range(NG):
+                eng.dma_start(out=inf_rows[4 * h:4 * h + 4, :].rearrange("t (u r) -> t u r", r=4), in_=rows[h])
 
-        def h_words(g, k):
-            return hw0[:, k, :] if g == 0 else hw12[:, k, (g - 1) * 2 * W:g * 2 * W]
+        def load_hw(g):
+            nc.sync.dma_start(out=hw[g][:].bitcast(I32), in_=hw_hbm[:, :, 2 * W * g:2 * W * (g + 1)].bitcast(I32))
 
         def spread_imports():
             imp_ps = psum.tile([P, 4, P], F32, name="imp_ps", tag="p", bufs=PB)
@@ -104,48 +108,29 @@ def tile_heat_contact_step_h2_kernel(tc, x_words, x_scales, heat_words, heat_sca
                                     rhs=idle_w[:].bitcast(FP8X4), rhs_scale=idle_s[:], start=True, stop=True)
 
         def inf_cast():
-            nc.vector.tensor_copy(out=inf_sq[:, 0:16].rearrange("p (h t i) -> p h t i", t=4, i=2),
-                                  in_=inf_raw[:, :, 0:4].unsqueeze(3).to_broadcast([P, NG, 4, 2]))
+            nc.vector.tensor_copy(out=inf_sq[:], in_=inf_rows[:])
 
-        def inf_turn_pe():
-            inf_bank[1] = psum.tile([P, P], F32, name="t_ps", tag="p", bufs=PB)
-            nc.tensor.transpose(inf_bank[1][:], inf_sq[:], ident[:])
+        def inf_turn():
+            inf_bank[0] = psum.tile([P, P], F32, name="inf_ps", tag="p", bufs=PB)
+            nc.tensor.transpose(inf_bank[0][:], inf_sq[:], ident[:])
 
-        def inf_turn_copy():
-            nc.scalar.copy(out=inf_t[:], in_=inf_bank[1][:])
+        def inf_copy():
+            nc.scalar.copy(out=inf[:], in_=inf_bank[0][:, 0:4 * NG].unsqueeze(2).to_broadcast([P, 4 * NG, 2]))
 
-        def inf_back():
-            inf_bank[0] = psum.tile([P, P], F32, name="inf_ps", tag="inf", bufs=1)
-            nc.tensor.transpose(inf_bank[0][:], inf_t[:], ident[:])
+        def perm_words(h, lo=0, hi=4):
+            nc.vector.tensor_copy(out=xw[h][:, lo:hi, :, :].rearrange("p t k (u r) -> p t (k u) r", r=4),
+                                  in_=xw_raw[h][:].rearrange("p k (u t r) -> p t (k u) r", t=4, r=4)[:, lo:hi, :, :])
 
-        def perm(dst, src):
-            nc.vector.tensor_copy(out=dst.rearrange("p k (t m) -> p t k m", t=4),
-                                  in_=src.rearrange("p k (m t) -> p t k m", t=4))
+        def perm_scales(h):
+            nc.vector.tensor_copy(out=xs[h][:].bitcast(I32).rearrange("p t k u -> p k u t"),
+                                  in_=xs_raw[:, :, h * W:(h + 1) * W].bitcast(I32).rearrange("p k (u t) -> p k u t", t=4))
 
-        def perm_words(h, k0=0, k1=NR):
-            for k in range(k0, k1):
-                nc.vector.tensor_copy(out=xw[h][:, k, :].rearrange("p (u e m) -> p u m e", u=2, e=2),
-                                      in_=xw_raw[h][:, k, :].rearrange("p (m u e) -> p u m e", u=2, e=2))
-
-        def perm_scales(h, k0=0, k1=NR):
-            perm(xs[h][:, k0:k1, :], xs_raw[:, k0:k1, h * W:(h + 1) * W])
-
-        def make_imprec(eng, g, s, b=None):
-            if b is None:
-                both = flow.tile([P, G], F32, name="imprec2", bufs=12)
-                imprec[g, 0, s], imprec[g, 1, s] = both[:, 0:W], both[:, W:G]
-                dst, src = both[:], imp_row[:]
-            else:
-                one = flow.tile([P, W], F32, name="imprec", bufs=1)
-                imprec[g, b, s] = one[:]
-                dst, src = one[:], imp_row[:, b * W:(b + 1) * W]
+        def make_imprec(eng, g, s, lo=0, hi=G):
+            dst, src = imprec[g][:, s, lo:hi], imp_row[:, lo:hi]
             if eng is S:
                 nc.scalar.activation(out=dst, in_=src, func=ACT.Copy, scale=rec[:, g, s:s + 1])
-            elif eng is V:
-                nc.vector.tensor_scalar(out=dst, in0=src, scalar1=rec[:, g, s:s + 1], scalar2=None, op0=ALU.mult)
             else:
-                nc.gpsimd.tensor_scalar(out=dst, in0=src, scalar1=rec[:, g, s:s + 1], scalar2=0.0,
-                                        op0=ALU.mult, op1=ALU.add)
+                nc.vector.tensor_scalar(out=dst, in0=src, scalar1=rec[:, g, s:s + 1], scalar2=None, op0=ALU.mult)
 
         def cti_out(t, run):
             return t.rearrange("p (c i) t -> p c t i", i=run)
@@ -154,24 +139,20 @@ def tile_heat_contact_step_h2_kernel(tc, x_words, x_scales, heat_words, heat_sca
             return t.rearrange("p t (c i) -> p c t i", i=run)
 
         def weave(eng, dst, src, lo, hi, run):
-            if eng is GP:
-                nc.gpsimd.tensor_scalar(out=cti_out(dst[:, lo:hi, :], run), in0=cti_in(src[:, :, lo:hi], run),
-                                        scalar1=1.0, scalar2=0.0, op0=ALU.mult, op1=ALU.add)
-            else:
-                copy = nc.scalar.copy if eng is S else nc.vector.tensor_copy
-                copy(out=cti_out(dst[:, lo:hi, :], run), in_=cti_in(src[:, :, lo:hi], run))
+            copy = nc.scalar.copy if eng is S else nc.vector.tensor_copy
+            copy(out=cti_out(dst[:, lo:hi, :], run), in_=cti_in(src[:, :, lo:hi], run))
 
         def weave_y(eng, g, b, lo=0, hi=W):
-            weave(eng, y_bf[g, b], y[g, b], lo, hi, 2)
+            weave(eng, y_bf[g][:, b * W:(b + 1) * W, :], y[g, b], lo, hi, 2)
 
         def weave_c(eng, h, b, lo=0, hi=W):
-            weave(eng, c_bf[h, b], c_raw[h][:, :, b * W:(b + 1) * W], lo, hi, 4)
+            weave(eng, c_bf[b][:, h, :, :], c_raw[h][:, :, b * W:(b + 1) * W], lo, hi, 4)
 
         def quant(src, words, scales):
             nc.vector.quantize_mx(out=words.bitcast(FP8X4), scales=scales, in_=src.rearrange("p n t -> p (n t)"))
 
-        def quant_c(h, b):
-            quant(c_bf[h, b][:], cw[h, b][:], cs[h, b][:])
+        def quant_c(b, lo=0, hi=G):
+            quant(c_bf[b][:].rearrange("p h n t -> p (h n) t")[:, lo:hi, :], cw[b][:, lo:hi], cs[b][:, lo:hi])
 
         def h_scales(g, k):
             return hs0[:, k, :] if g == 0 else hs12[:, k, (g - 1) * W:g * W]
@@ -179,9 +160,8 @@ def tile_heat_contact_step_h2_kernel(tc, x_words, x_scales, heat_words, heat_sca
         def spread_pass(g, h, t, k):
             if k == 0:
                 d_ps[g, h, t] = psum.tile([P, W], F32, name="d_ps", tag=DTAG, bufs=DB)
-            cols = slice(t * P, (t + 1) * P)
-            nc.tensor.matmul_mx(out=d_ps[g, h, t][:], lhsT=xw[h][:, k, cols].bitcast(FP8X4), lhsT_scale=xs[h][:, k, cols],
-                                rhs=h_words(g, k).bitcast(FP4X4), rhs_scale=h_scales(g, k),
+            nc.tensor.matmul_mx(out=d_ps[g, h, t][:], lhsT=xw[h][:, t, k, :].bitcast(FP8X4), lhsT_scale=xs[h][:, t, k, :],
+                                rhs=hw[g][:, k, :].bitcast(FP4X4), rhs_scale=h_scales(g, k),
                                 start=(k == 0), stop=(k == NR - 1))
 
         def spread(g, h, ts=(0, 1, 2, 3)):
@@ -189,165 +169,198 @@ def tile_heat_contact_step_h2_kernel(tc, x_words, x_scales, heat_words, heat_sca
                 for k in range(NR):
                     spread_pass(g, h, t, k)
 
-        def spread_first():
-            for t in range(4):
-                spread_pass(0, 0, t, 0)
-            for t in range(4):
-                spread_pass(0, 0, t, 1)
-                spread_pass(0, 0, t, 2)
-
         def tanh(g, h, ts=(0, 1, 2, 3)):
             for t in ts:
                 if t == 0:
                     th[g, h] = flow.tile([P, 4, W], F32, name="th", bufs=3, align_bytes=64)
+                    if h == 0:
+                        z_bf[g] = flow.tile([P, NG * W, 4], BF16, name="z_bf", bufs=2, align_bytes=64)
                 nc.scalar.activation(out=th[g, h][:, t, :].rearrange("p (s m) -> p s m", s=4),
                                      in_=d_ps[g, h, t][:].rearrange("p (m s) -> p s m", s=4), func=ACT.Tanh)
 
-        def weigh(g, h, from_psum=False):
-            src = inf_bank[0] if from_psum else inf_sq
-            fac = src[:, 8 * h:8 * h + 8].rearrange("p (t i) -> p t i", i=2).unsqueeze(1)
-            z_bf[g, h] = flow.tile([P, W, 4], BF16, name="z_bf", bufs=2, align_bytes=64)
-            nc.vector.tensor_tensor(out=cti_out(z_bf[g, h][:], 2), in0=cti_in(th[g, h][:], 2),
-                                    in1=fac.to_broadcast([P, W // 2, 4, 2]), op=ALU.mult)
+        def weigh(g, h, lo=0, hi=W):
+            fac = inf[:, 4 * h:4 * h + 4, :].unsqueeze(1)
+            nc.vector.tensor_tensor(out=cti_out(z_bf[g][:, h * W + lo:h * W + hi, :], 2),
+                                    in0=cti_in(th[g, h][:, :, lo:hi], 2),
+                                    in1=fac.to_broadcast([P, (hi - lo) // 2, 4, 2]), op=ALU.mult)
 
-        def quant_z(g, h):
-            quant(z_bf[g, h][:], zw[g, h][:], zs[g, h][:])
+        def weigh_rows(g, h, ts, lo=0, hi=W):
+            for t in ts:
+                nc.scalar.activation(out=z_rows[:, t, lo:hi], in_=th[g, h][:, t, lo:hi], func=ACT.Copy,
+                                     scale=inf[:, 4 * h + t, 0:1])
+
+        def weave_z(eng, g, h, lo=0, hi=W):
+            weave(eng, z_bf[g][:, h * W:(h + 1) * W, :], z_rows, lo, hi, 4)
+
+        def quant_z(g, lo=0, hi=G):
+            quant(z_bf[g][:, lo:hi, :], zw[g][:, lo:hi], zs[g][:, lo:hi])
 
         def contact(g, b, ss=(0, 1, 2, 3)):
             for s in ss:
                 p_ps[g, b, s] = psum.tile([P, W], F32, name="p_ps", tag="p", bufs=PB)
-                cols = slice(s * P, (s + 1) * P)
                 for h in range(NG):
-                    nc.tensor.matmul_mx(out=p_ps[g, b, s][:], lhsT=zw[g, h][:, cols].bitcast(FP8X4),
-                                        lhsT_scale=zs[g, h][:, cols],
-                                        rhs=cw[h, b][:].bitcast(FP8X4), rhs_scale=cs[h, b][:],
+                    regions = slice(h * W + s * P, h * W + (s + 1) * P)
+                    groups = slice(h * W, (h + 1) * W)
+                    nc.tensor.matmul_mx(out=p_ps[g, b, s][:], lhsT=zw[g][:, regions].bitcast(FP8X4),
+                                        lhsT_scale=zs[g][:, regions],
+                                        rhs=cw[b][:, groups].bitcast(FP8X4), rhs_scale=cs[b][:, groups],
                                         start=(h == 0), stop=(h == NG - 1))
 
-        def finish(g, b, then=None):
-            y[g, b] = flow.tile([P, 4, W], F32, name="y", bufs=3, align_bytes=64)
-            y_bf[g, b] = flow.tile([P, W, 4], BF16, name="y_bf", bufs=3, align_bytes=64)
+        def finish(g, b, ss=(0, 1, 2, 3), lo=0, hi=W, join=1):
+            if ss[0] == 0 and lo == 0:
+                y[g, b] = flow.tile([P, 4, W], F32, name="y", tag="y", bufs=4, align_bytes=64)
+                if b == 0:
+                    y_bf[g] = flow.tile([P, G, 4], BF16, name="y_bf", tag="y_bf", bufs=2, align_bytes=64)
             rows = out_0[g * W:(g + 1) * W, b * W:(b + 1) * W].rearrange("(p s) n -> p s n", s=4)
-            for s in range(4):
-                nc.vector.scalar_tensor_tensor(out=y[g, b][:, s, :], in0=p_ps[g, b, s][:], scalar=rec[:, g, s:s + 1],
-                                               in1=imprec[g, b, s], op0=ALU.mult, op1=ALU.add)
-                nc.sync.dma_start(out=rows[:, s, :], in_=y[g, b][:, s, :])
-                if then is not None:
-                    make_imprec(GP, then[0], s, then[1])
+            for s in ss:
+                nc.vector.scalar_tensor_tensor(out=y[g, b][:, s, lo:hi], in0=p_ps[g, b, s][:, lo:hi],
+                                               scalar=rec[:, g, s:s + 1], in1=imprec[g][:, s, b * W + lo:b * W + hi],
+                                               op0=ALU.mult, op1=ALU.add)
+                if (s + 1) % join == 0:
+                    nc.sync.dma_start(out=rows[:, s + 1 - join:s + 1, lo:hi], in_=y[g, b][:, s + 1 - join:s + 1, lo:hi])
 
-        def store_scales(gs):
+        def store_scales(gs, lo, hi):
             for q in range(4):
-                nc.sync.dma_start(out=out_2[gs, 4 * q:4 * q + 4, :].rearrange("g r n -> r g n").bitcast(I32),
-                                  in_=ys[32 * q:32 * q + 4, gs, :].bitcast(I32))
+                nc.sync.dma_start(out=out_2[gs, 4 * q:4 * q + 4, lo:hi].rearrange("g r n -> r g n").bitcast(I32),
+                                  in_=ys[32 * q:32 * q + 4, gs, lo:hi].bitcast(I32))
 
-        def quant_y(g, b):
-            yw = flow.tile([P, W], I32, name="yw", bufs=3, align_bytes=64)
-            quant(y_bf[g, b][:], yw[:], ys[:, g, b * W:(b + 1) * W])
-            nc.sync.dma_start(out=yw_hbm[g, :, 4 * W * b:4 * W * (b + 1)].bitcast(I32), in_=yw[:])
+        def quant_y(g, lo=0, hi=G):
+            quant(y_bf[g][:, lo:hi, :], yw[g][:, lo:hi], ys[:, g, lo:hi])
+            nc.sync.dma_start(out=yw_hbm[g, :, 4 * lo:4 * hi].bitcast(I32), in_=yw[g][:, lo:hi])
 
-        nc.vector.memset(warm[:, 0:8], 0.0)
+        nc.gpsimd.memset(warm[:, 0:8], 0.0)
         nc.vector.memset(hs0[:].bitcast(I32), 0)
         nc.vector.memset(xs_raw[:].bitcast(I32), 0)
         nc.scalar.activation(out=warm[:, 8:16], in_=warm[:, 0:8], func=ACT.Tanh)
         nc.sync.dma_start(out=imp_col[:], in_=imports.rearrange("(n m) -> n m", m=8))
         nc.sync.dma_start(out=rec_raw[:, :, 0:4], in_=recovery.rearrange("(g p s) -> p g s", p=P, s=4))
         load_x(0)
-        load_hw(hw0, 0, 1)
+        load_hw(0)
         make_identity(nc, ident[:])
         scale_rows(nc.gpsimd, hs0, heat_scales, slice(0, W), (2, 3))
         scale_rows(nc.sync, xs_raw, x_scales, slice(0, G))
         scale_rows(nc.sync, hs0, heat_scales, slice(0, W), (0, 1))
-        load_x(1)
         nc.vector.memset(idle_bf[:].bitcast(I32), 0)
         nc.vector.quantize_mx(out=idle_w[:].bitcast(FP8X4), scales=idle_s[:], in_=idle_bf[:])
         nc.vector.memset(hs12[:].bitcast(I32), 0)
+        nc.vector.memset(inf_rows[:].bitcast(I32), 0)
         nc.vector.tensor_copy(out=rec[:], in_=rec_raw[:, :, 0:4])
-        nc.sync.dma_start(out=inf_raw[:, :, 0:4], in_=infectivity.rearrange("(h p t) -> p h t", p=P, t=4))
-        load_c(0)
-        scale_rows(nc.sync, hs12, heat_scales, slice(W, R))
-        load_hw(hw12, 1, 3)
-        load_c(1)
 
         H = W // 2
         spread_imports()
         warm_tensor(18)
-        for k in range(NR):
-            perm_words(0, k, k + 1)
-        for k in range(NR):
-            perm_scales(0, k, k + 1)
-        spread(0, 0)
-        perm_scales(1)
-        for s in range(3):
-            make_imprec(S, 0, s)
-        make_imprec(V, 2, 1)
-        perm_words(1)
-        inf_cast()
-        make_imprec(V, 0, 3)
-        tanh(0, 0)
-        spread(0, 1)
-        weigh(0, 0)
-        weave_c(V, 0, 0)
-        quant_z(0, 0)
-        quant_c(0, 0)
-        tanh(0, 1, (0, 1))
-        weave_c(S, 0, 1, 0, H)
-        tanh(0, 1, (2, 3))
-        weave_c(S, 0, 1, H, W)
-        spread(1, 0)
-        weigh(0, 1)
-        weave_c(V, 1, 0)
-        quant_z(0, 1)
-        quant_c(1, 0)
-        tanh(1, 0, (0, 1))
-        weave_c(S, 1, 1, 0, H)
-        tanh(1, 0, (2, 3))
-        spread(1, 1)
-        contact(0, 0)
-        weigh(1, 0)
-        quant_c(0, 1)
-        quant_z(1, 0)
-        weave_c(S, 1, 1, H, W)
-        make_imprec(S, 1, 0)
+        make_imprec(S, 0, 0)
+        make_imprec(V, 1, 2)
+        load_x(1)
+        perm_words(0)
+        load_inf(nc.sync)
         make_imprec(S, 1, 1)
-        finish(0, 0)
-        quant_c(1, 1)
-        tanh(1, 1)
-        spread(2, 0)
-        contact(0, 1)
-        weigh(1, 1)
-        make_imprec(S, 1, 2)
+        load_c(0)
+        perm_scales(0)
+        make_imprec(V, 1, 0)
+        load_hw(1)
+        spread(0, 0, (0, 1))
+        make_imprec(S, 2, 3)
+        make_imprec(V, 2, 0)
+        make_imprec(V, 0, 3)
+        tanh(0, 0, (0, 1))
+        make_imprec(V, 0, 2)
+        spread(0, 0, (2, 3))
+        scale_rows(nc.sync, hs12, heat_scales, slice(W, R))
+        make_imprec(V, 0, 1)
+        tanh(0, 0, (2, 3))
+        inf_cast()
+        perm_scales(1)
+        perm_words(1)
+        inf_turn()
+        load_c(1)
+        inf_copy()
+        spread(0, 1, (0, 1))
+        weigh(0, 0)
+        weave_c(S, 0, 1)
+        load_hw(2)
+        spread(0, 1, (2, 3))
+        weave_c(V, 0, 0)
+        tanh(0, 1, (0, 1))
+        spread(1, 0, (0, 1))
+        quant_z(0, 0, W)
+        tanh(0, 1, (2, 3))
+        quant_c(1, 0, W)
+        quant_c(0, 0, W)
+        tanh(1, 0, (0, 1))
+        spread(1, 0, (2, 3))
+        weave_c(V, 1, 0, H, W)
+        weigh(0, 1)
+        weave_c(S, 1, 0, 0, H)
+        spread(1, 1, (0, 1))
+        tanh(1, 0, (2, 3))
+        quant_c(0, W, G)
+        spread(1, 1, (2, 3))
+        weave_c(S, 1, 1)
+        quant_z(0, W, G)
+        weigh(1, 0)
+        contact(0, 0, (0, 1))
+        tanh(1, 1, (0, 1))
+        contact(0, 0, (2, 3))
+        finish(0, 0, (0, 1))
         make_imprec(S, 1, 3)
-        tanh(2, 0)
-        finish(0, 1)
-        quant_z(1, 1)
-        spread(2, 1)
-        contact(1, 0)
+        spread(2, 0, (0, 1))
+        quant_c(1, W, G)
+        tanh(1, 1, (2, 3))
+        finish(0, 0, (2, 3))
+        contact(0, 1, (0, 1))
+        tanh(2, 0, (0, 1))
+        quant_z(1, 0, W)
+        spread(2, 1, (0, 1))
+        finish(0, 1, (0, 1))
         weave_y(S, 0, 0)
-        weigh(2, 0)
-        quant_y(0, 0)
-        quant_z(2, 0)
-        weave_y(S, 0, 1)
-        tanh(2, 1)
-        finish(1, 0)
-        contact(1, 1)
-        make_imprec(S, 2, 0)
+        weigh(1, 1)
+        contact(0, 1, (2, 3))
+        weigh_rows(2, 0, (0, 1))
+        spread(2, 0, (2, 3))
+        quant_y(0, 0, W)
+        tanh(2, 1, (0, 1))
+        quant_z(1, W, G)
+        contact(1, 0, (0, 1))
+        finish(0, 1, (2, 3))
+        tanh(2, 0, (2, 3))
+        contact(1, 1, (0, 1))
+        finish(1, 0, (0, 1))
+        weave_y(S, 0, 1, 0, H)
+        spread(2, 1, (2, 3))
+        weave_y(V, 0, 1, H, W)
+        weigh_rows(2, 0, (2, 3))
+        finish(1, 1, (0, 1))
+        tanh(2, 1, (2, 3))
+        contact(1, 0, (2, 3))
+        quant_y(0, W, G)
+        finish(1, 0, (2, 3))
+        contact(1, 1, (2, 3))
+        weave_z(S, 2, 0)
+        store_scales(slice(0, 1), 0, G)
         weigh(2, 1)
         weave_y(S, 1, 0)
-        quant_y(0, 1)
-        store_scales(slice(0, 1))
-        quant_z(2, 1)
+        quant_z(2, 0, W)
+        quant_z(2, W, G)
+        contact(2, 0, (0, 1))
+        make_imprec(S, 2, 1)
+        finish(1, 1, (2, 3))
         make_imprec(S, 2, 2)
-        make_imprec(S, 2, 3)
-        finish(1, 1)
-        contact(2, 0)
+        quant_y(1, 0, W)
+        finish(2, 0, (0, 1))
+        contact(2, 0, (2, 3))
         weave_y(S, 1, 1)
-        quant_y(1, 0)
-        finish(2, 0)
-        contact(2, 1)
+        contact(2, 1, (0, 1))
+        finish(2, 0, (2, 3))
+        contact(2, 1, (2, 3))
+        finish(2, 1, (0, 1))
         weave_y(S, 2, 0)
-        quant_y(1, 1)
-        finish(2, 1)
-        quant_y(2, 0)
-        weave_y(V, 2, 1, 0, 320)
-        weave_y(S, 2, 1, 320, W)
-        quant_y(2, 1)
-        store_scales(slice(1, 3))
+        finish(2, 1, (2, 3))
+        quant_y(1, W, G)
+        weave_y(S, 2, 1, 0, H)
+        quant_y(2, 0, W)
+        weave_y(V, 2, 1, H, 416)
+        weave_y(S, 2, 1, 416, W)
+        quant_y(2, W, W + H)
+        quant_y(2, W + H, G)
+        store_scales(slice(1, 3), 0, G)

from contextlib import ExitStack

import concourse.mybir as mybir
from concourse.masks import make_identity

R, G = 1536, 1024
FLOPS = 2 * R * R * G + 2 * R * G * G

F32 = mybir.dt.float32
BF16 = mybir.dt.bfloat16
I32 = mybir.dt.int32
U8 = mybir.dt.uint8
FP8X4 = mybir.dt.float8_e4m3fn_x4
FP4X4 = mybir.dt.float4_e2m1fn_x4
ACT = mybir.ActivationFunctionType
ALU = mybir.AluOpType

P = 128
W = 512
NR = R // W
NG = G // W
PB = 4
DB = 4
DTAG = "d"


def tile_heat_contact_step_h2_kernel(tc, x_words, x_scales, heat_words, heat_scales,
                                                infectivity, contacts, imports, recovery,
                                                out_0, out_1, out_2):
    nc = tc.nc
    S, V = nc.scalar, nc.vector
    with ExitStack() as ctx:
        keep = ctx.enter_context(tc.tile_pool(name="keep", bufs=1))
        flow = ctx.enter_context(tc.tile_pool(name="flow", bufs=2))
        psum = ctx.enter_context(tc.psum_pool(name="psum", bufs=4))
        ctx.enter_context(tc.manual_schedule())

        def kt(name, shape, dt):
            return keep.tile(shape, dt, name=name, align_bytes=64)

        ident = kt("ident", [P, P], F32)
        warm = kt("warm", [P, 16], F32)
        imp_col = kt("imp_col", [P, 8], BF16)
        imp_row = kt("imp_row", [P, G], BF16)
        rec_raw = kt("rec_raw", [P, NR, 16], BF16)
        rec = kt("rec", [P, NR, 4], F32)
        inf_rows = kt("inf_rows", [P, P], BF16)
        inf_sq = kt("inf_sq", [P, P], F32)
        inf = kt("inf", [P, 4 * NG, 2], F32)
        xs_raw = kt("xs_raw", [P, NR, G], U8)
        hs0 = kt("hs0", [P, NR, W], U8)
        xs = [kt("xs%d" % h, [P, 4, NR, P], U8) for h in range(NG)]
        xw_raw = [flow.tile([P, NR, W], I32, name="xw_raw%d" % h, tag="y", bufs=4, align_bytes=64) for h in range(NG)]
        xw = [kt("xw%d" % h, [P, 4, NR, P], I32) for h in range(NG)]
        hw = [kt("hw%d" % g, [P, NR, 2 * W], U8) for g in range(NR)]
        hs12 = kt("hs12", [P, NR, 2 * W], U8)
        c_raw = [flow.tile([P, 4, G], BF16, name="c_raw%d" % h, tag="y_bf", bufs=2, align_bytes=64) for h in range(NG)]
        c_bf = [kt("c_bf%d" % b, [P, NG, W, 4], BF16) for b in range(NG)]
        cw = [kt("cw%d" % b, [P, NG * W], I32) for b in range(NG)]
        cs = [kt("cs%d" % b, [P, NG * W], U8) for b in range(NG)]
        zw = [kt("zw%d" % g, [P, NG * W], I32) for g in range(NR)]
        zs = [kt("zs%d" % g, [P, NG * W], U8) for g in range(NR)]
        yw = [kt("yw%d" % g, [P, G], I32) for g in range(NR)]
        imprec = [kt("imprec%d" % g, [P, 4, G], F32) for g in range(NR)]
        z_rows = kt("z_rows", [P, 4, W], BF16)
        idle_bf = kt("idle_bf", [P, 4 * P], BF16)
        idle_w = kt("idle_w", [P, P], I32)
        idle_s = kt("idle_s", [P, P], U8)
        ys = kt("ys", [P, NR, G], U8)
        inf_bank, d_ps, th, z_bf, p_ps, y, y_bf = {}, {}, {}, {}, {}, {}, {}

        xw_hbm = x_words.rearrange("g p n t -> p g (n t)")
        hw_hbm = heat_words.rearrange("g p n -> p g n")
        yw_hbm = out_1.rearrange("g p n t -> g p (n t)")

        def scale_rows(eng, tile_ap, hbm, cols, qs=(0, 1, 2, 3)):
            for q in qs:
                eng.dma_start(out=tile_ap[32 * q:32 * q + 4, :, :].bitcast(I32),
                              in_=hbm[:, 4 * q:4 * q + 4, cols].rearrange("g r n -> r g n").bitcast(I32))

        def load_x(h):
            nc.sync.dma_start(out=xw_raw[h][:], in_=xw_hbm[:, :, 4 * W * h:4 * W * (h + 1)].bitcast(I32))

        def load_c(h, lo=0, hi=G):
            rows = contacts[h * W:(h + 1) * W, :].rearrange("(u t r) n -> r u t n", t=4, r=4)
            for r in range(4):
                nc.sync.dma_start(out=c_raw[h][r:P:4, :, lo:hi], in_=rows[r][:, :, lo:hi])

        def load_inf(eng):
            rows = infectivity.rearrange("(h u t r) -> h t u r", h=NG, t=4, r=4)
            for h in range(NG):
                eng.dma_start(out=inf_rows[4 * h:4 * h + 4, :].rearrange("t (u r) -> t u r", r=4), in_=rows[h])

        def load_hw(g):
            nc.sync.dma_start(out=hw[g][:].bitcast(I32), in_=hw_hbm[:, :, 2 * W * g:2 * W * (g + 1)].bitcast(I32))

        def spread_imports():
            imp_ps = psum.tile([P, 4, P], F32, name="imp_ps", tag="p", bufs=PB)
            for m in range(4):
                nc.tensor.transpose(imp_ps[:, m, :], imp_col[:].bitcast(F32)[:, m:m + 1].to_broadcast([P, P]), ident[:])
            nc.scalar.copy(out=imp_row[:].bitcast(F32).rearrange("p (n m) -> p n m", m=4),
                           in_=imp_ps[:].rearrange("p m n -> p n m"))

        def warm_tensor(n):
            idle_ps = psum.tile([P, P], F32, name="idle_ps", tag="p", bufs=PB)
            for i in range(n):
                nc.tensor.matmul_mx(out=idle_ps[:], lhsT=idle_w[:].bitcast(FP8X4), lhsT_scale=idle_s[:],
                                    rhs=idle_w[:].bitcast(FP8X4), rhs_scale=idle_s[:], start=True, stop=True)

        def inf_cast():
            nc.vector.tensor_copy(out=inf_sq[:], in_=inf_rows[:])

        def inf_turn():
            inf_bank[0] = psum.tile([P, P], F32, name="inf_ps", tag="p", bufs=PB)
            nc.tensor.transpose(inf_bank[0][:], inf_sq[:], ident[:])

        def inf_copy():
            nc.scalar.copy(out=inf[:], in_=inf_bank[0][:, 0:4 * NG].unsqueeze(2).to_broadcast([P, 4 * NG, 2]))

        def perm_words(h, lo=0, hi=4):
            nc.vector.tensor_copy(out=xw[h][:, lo:hi, :, :].rearrange("p t k (u r) -> p t (k u) r", r=4),
                                  in_=xw_raw[h][:].rearrange("p k (u t r) -> p t (k u) r", t=4, r=4)[:, lo:hi, :, :])

        def perm_scales(h):
            nc.vector.tensor_copy(out=xs[h][:].bitcast(I32).rearrange("p t k u -> p k u t"),
                                  in_=xs_raw[:, :, h * W:(h + 1) * W].bitcast(I32).rearrange("p k (u t) -> p k u t", t=4))

        def make_imprec(eng, g, s, lo=0, hi=G):
            dst, src = imprec[g][:, s, lo:hi], imp_row[:, lo:hi]
            if eng is S:
                nc.scalar.activation(out=dst, in_=src, func=ACT.Copy, scale=rec[:, g, s:s + 1])
            else:
                nc.vector.tensor_scalar(out=dst, in0=src, scalar1=rec[:, g, s:s + 1], scalar2=None, op0=ALU.mult)

        def cti_out(t, run):
            return t.rearrange("p (c i) t -> p c t i", i=run)

        def cti_in(t, run):
            return t.rearrange("p t (c i) -> p c t i", i=run)

        def weave(eng, dst, src, lo, hi, run):
            copy = nc.scalar.copy if eng is S else nc.vector.tensor_copy
            copy(out=cti_out(dst[:, lo:hi, :], run), in_=cti_in(src[:, :, lo:hi], run))

        def weave_y(eng, g, b, lo=0, hi=W):
            weave(eng, y_bf[g][:, b * W:(b + 1) * W, :], y[g, b], lo, hi, 2)

        def weave_c(eng, h, b, lo=0, hi=W):
            weave(eng, c_bf[b][:, h, :, :], c_raw[h][:, :, b * W:(b + 1) * W], lo, hi, 4)

        def quant(src, words, scales):
            nc.vector.quantize_mx(out=words.bitcast(FP8X4), scales=scales, in_=src.rearrange("p n t -> p (n t)"))

        def quant_c(b, lo=0, hi=G):
            quant(c_bf[b][:].rearrange("p h n t -> p (h n) t")[:, lo:hi, :], cw[b][:, lo:hi], cs[b][:, lo:hi])

        def h_scales(g, k):
            return hs0[:, k, :] if g == 0 else hs12[:, k, (g - 1) * W:g * W]

        def spread_pass(g, h, t, k):
            if k == 0:
                d_ps[g, h, t] = psum.tile([P, W], F32, name="d_ps", tag=DTAG, bufs=DB)
            nc.tensor.matmul_mx(out=d_ps[g, h, t][:], lhsT=xw[h][:, t, k, :].bitcast(FP8X4), lhsT_scale=xs[h][:, t, k, :],
                                rhs=hw[g][:, k, :].bitcast(FP4X4), rhs_scale=h_scales(g, k),
                                start=(k == 0), stop=(k == NR - 1))

        def spread(g, h, ts=(0, 1, 2, 3)):
            for t in ts:
                for k in range(NR):
                    spread_pass(g, h, t, k)

        def tanh(g, h, ts=(0, 1, 2, 3)):
            for t in ts:
                if t == 0:
                    th[g, h] = flow.tile([P, 4, W], F32, name="th", bufs=3, align_bytes=64)
                    if h == 0:
                        z_bf[g] = flow.tile([P, NG * W, 4], BF16, name="z_bf", bufs=2, align_bytes=64)
                nc.scalar.activation(out=th[g, h][:, t, :].rearrange("p (s m) -> p s m", s=4),
                                     in_=d_ps[g, h, t][:].rearrange("p (m s) -> p s m", s=4), func=ACT.Tanh)

        def weigh(g, h, lo=0, hi=W):
            fac = inf[:, 4 * h:4 * h + 4, :].unsqueeze(1)
            nc.vector.tensor_tensor(out=cti_out(z_bf[g][:, h * W + lo:h * W + hi, :], 2),
                                    in0=cti_in(th[g, h][:, :, lo:hi], 2),
                                    in1=fac.to_broadcast([P, (hi - lo) // 2, 4, 2]), op=ALU.mult)

        def weigh_rows(g, h, ts, lo=0, hi=W):
            for t in ts:
                nc.scalar.activation(out=z_rows[:, t, lo:hi], in_=th[g, h][:, t, lo:hi], func=ACT.Copy,
                                     scale=inf[:, 4 * h + t, 0:1])

        def weave_z(eng, g, h, lo=0, hi=W):
            weave(eng, z_bf[g][:, h * W:(h + 1) * W, :], z_rows, lo, hi, 4)

        def quant_z(g, lo=0, hi=G):
            quant(z_bf[g][:, lo:hi, :], zw[g][:, lo:hi], zs[g][:, lo:hi])

        def contact(g, b, ss=(0, 1, 2, 3)):
            for s in ss:
                p_ps[g, b, s] = psum.tile([P, W], F32, name="p_ps", tag="p", bufs=PB)
                for h in range(NG):
                    regions = slice(h * W + s * P, h * W + (s + 1) * P)
                    groups = slice(h * W, (h + 1) * W)
                    nc.tensor.matmul_mx(out=p_ps[g, b, s][:], lhsT=zw[g][:, regions].bitcast(FP8X4),
                                        lhsT_scale=zs[g][:, regions],
                                        rhs=cw[b][:, groups].bitcast(FP8X4), rhs_scale=cs[b][:, groups],
                                        start=(h == 0), stop=(h == NG - 1))

        def finish(g, b, ss=(0, 1, 2, 3), lo=0, hi=W, join=1):
            if ss[0] == 0 and lo == 0:
                y[g, b] = flow.tile([P, 4, W], F32, name="y", tag="y", bufs=4, align_bytes=64)
                if b == 0:
                    y_bf[g] = flow.tile([P, G, 4], BF16, name="y_bf", tag="y_bf", bufs=2, align_bytes=64)
            rows = out_0[g * W:(g + 1) * W, b * W:(b + 1) * W].rearrange("(p s) n -> p s n", s=4)
            for s in ss:
                nc.vector.scalar_tensor_tensor(out=y[g, b][:, s, lo:hi], in0=p_ps[g, b, s][:, lo:hi],
                                               scalar=rec[:, g, s:s + 1], in1=imprec[g][:, s, b * W + lo:b * W + hi],
                                               op0=ALU.mult, op1=ALU.add)
                if (s + 1) % join == 0:
                    nc.sync.dma_start(out=rows[:, s + 1 - join:s + 1, lo:hi], in_=y[g, b][:, s + 1 - join:s + 1, lo:hi])

        def store_scales(gs, lo, hi):
            for q in range(4):
                nc.sync.dma_start(out=out_2[gs, 4 * q:4 * q + 4, lo:hi].rearrange("g r n -> r g n").bitcast(I32),
                                  in_=ys[32 * q:32 * q + 4, gs, lo:hi].bitcast(I32))

        def quant_y(g, lo=0, hi=G):
            quant(y_bf[g][:, lo:hi, :], yw[g][:, lo:hi], ys[:, g, lo:hi])
            nc.sync.dma_start(out=yw_hbm[g, :, 4 * lo:4 * hi].bitcast(I32), in_=yw[g][:, lo:hi])

        nc.gpsimd.memset(warm[:, 0:8], 0.0)
        nc.vector.memset(hs0[:].bitcast(I32), 0)
        nc.vector.memset(xs_raw[:].bitcast(I32), 0)
        nc.scalar.activation(out=warm[:, 8:16], in_=warm[:, 0:8], func=ACT.Tanh)
        nc.sync.dma_start(out=imp_col[:], in_=imports.rearrange("(n m) -> n m", m=8))
        nc.sync.dma_start(out=rec_raw[:, :, 0:4], in_=recovery.rearrange("(g p s) -> p g s", p=P, s=4))
        load_x(0)
        load_hw(0)
        make_identity(nc, ident[:])
        scale_rows(nc.gpsimd, hs0, heat_scales, slice(0, W), (2, 3))
        scale_rows(nc.sync, xs_raw, x_scales, slice(0, G))
        scale_rows(nc.sync, hs0, heat_scales, slice(0, W), (0, 1))
        nc.vector.memset(idle_bf[:].bitcast(I32), 0)
        nc.vector.quantize_mx(out=idle_w[:].bitcast(FP8X4), scales=idle_s[:], in_=idle_bf[:])
        nc.vector.memset(hs12[:].bitcast(I32), 0)
        nc.vector.memset(inf_rows[:].bitcast(I32), 0)
        nc.vector.tensor_copy(out=rec[:], in_=rec_raw[:, :, 0:4])

        H = W // 2
        spread_imports()
        warm_tensor(18)
        make_imprec(S, 0, 0)
        make_imprec(V, 1, 2)
        load_x(1)
        perm_words(0)
        load_inf(nc.sync)
        make_imprec(S, 1, 1)
        load_c(0)
        perm_scales(0)
        make_imprec(V, 1, 0)
        load_hw(1)
        spread(0, 0, (0, 1))
        make_imprec(S, 2, 3)
        make_imprec(V, 2, 0)
        make_imprec(V, 0, 3)
        tanh(0, 0, (0, 1))
        make_imprec(V, 0, 2)
        spread(0, 0, (2, 3))
        scale_rows(nc.sync, hs12, heat_scales, slice(W, R))
        make_imprec(V, 0, 1)
        tanh(0, 0, (2, 3))
        inf_cast()
        perm_scales(1)
        perm_words(1)
        inf_turn()
        load_c(1)
        inf_copy()
        spread(0, 1, (0, 1))
        weigh(0, 0)
        weave_c(S, 0, 1)
        load_hw(2)
        spread(0, 1, (2, 3))
        weave_c(V, 0, 0)
        tanh(0, 1, (0, 1))
        spread(1, 0, (0, 1))
        quant_z(0, 0, W)
        tanh(0, 1, (2, 3))
        quant_c(1, 0, W)
        quant_c(0, 0, W)
        tanh(1, 0, (0, 1))
        spread(1, 0, (2, 3))
        weave_c(V, 1, 0, H, W)
        weigh(0, 1)
        weave_c(S, 1, 0, 0, H)
        spread(1, 1, (0, 1))
        tanh(1, 0, (2, 3))
        quant_c(0, W, G)
        spread(1, 1, (2, 3))
        weave_c(S, 1, 1)
        quant_z(0, W, G)
        weigh(1, 0)
        contact(0, 0, (0, 1))
        tanh(1, 1, (0, 1))
        contact(0, 0, (2, 3))
        finish(0, 0, (0, 1))
        make_imprec(S, 1, 3)
        spread(2, 0, (0, 1))
        quant_c(1, W, G)
        tanh(1, 1, (2, 3))
        finish(0, 0, (2, 3))
        contact(0, 1, (0, 1))
        tanh(2, 0, (0, 1))
        quant_z(1, 0, W)
        spread(2, 1, (0, 1))
        finish(0, 1, (0, 1))
        weave_y(S, 0, 0)
        weigh(1, 1)
        contact(0, 1, (2, 3))
        weigh_rows(2, 0, (0, 1))
        spread(2, 0, (2, 3))
        quant_y(0, 0, W)
        tanh(2, 1, (0, 1))
        quant_z(1, W, G)
        contact(1, 0, (0, 1))
        finish(0, 1, (2, 3))
        tanh(2, 0, (2, 3))
        contact(1, 1, (0, 1))
        finish(1, 0, (0, 1))
        weave_y(S, 0, 1, 0, H)
        spread(2, 1, (2, 3))
        weave_y(V, 0, 1, H, W)
        weigh_rows(2, 0, (2, 3))
        finish(1, 1, (0, 1))
        tanh(2, 1, (2, 3))
        contact(1, 0, (2, 3))
        quant_y(0, W, G)
        finish(1, 0, (2, 3))
        contact(1, 1, (2, 3))
        weave_z(S, 2, 0)
        store_scales(slice(0, 1), 0, G)
        weigh(2, 1)
        weave_y(S, 1, 0)
        quant_z(2, 0, W)
        quant_z(2, W, G)
        contact(2, 0, (0, 1))
        make_imprec(S, 2, 1)
        finish(1, 1, (2, 3))
        make_imprec(S, 2, 2)
        quant_y(1, 0, W)
        finish(2, 0, (0, 1))
        contact(2, 0, (2, 3))
        weave_y(S, 1, 1)
        contact(2, 1, (0, 1))
        finish(2, 0, (2, 3))
        contact(2, 1, (2, 3))
        finish(2, 1, (0, 1))
        weave_y(S, 2, 0)
        finish(2, 1, (2, 3))
        quant_y(1, W, G)
        weave_y(S, 2, 1, 0, H)
        quant_y(2, 0, W)
        weave_y(V, 2, 1, H, 416)
        weave_y(S, 2, 1, 416, W)
        quant_y(2, W, W + H)
        quant_y(2, W + H, G)
        store_scales(slice(1, 3), 0, G)
